import numpy as np, ml_dtypes
CORES = [16,18,20,22]
N = 4
BF = ml_dtypes.bfloat16
def gentries(a):
    return np.ascontiguousarray(a.reshape(8, 16, -1).transpose(0, 2, 1)).reshape(8, -1)
def gtable(e):
    e = np.asarray(e); return np.ascontiguousarray(e.reshape(8, -1, 16).transpose(0, 2, 1)).reshape(128, -1).astype(np.int32)
F, M, T, H = 1024, 4, 5, 9
W = N * F
def pack(x, m, nm):
    return {"x": np.ascontiguousarray(x.reshape(128, N, F).transpose(1, 0, 2)).astype(BF), "mix": np.ascontiguousarray(m.reshape(16, N, F).transpose(1, 0, 2)).astype(BF),
            "nb": np.stack([gtable(np.ascontiguousarray(nm[:, q * F:(q + 1) * F].transpose(0, 2, 1)).reshape(8, -1)) for q in range(N)])}
def spaced(nm):
    nm = nm.astype(np.int64) % W; own = np.arange(W)[None, :]
    for j in range(M):
        for i in range(M + 1):
            clash = nm[:, :, j] == own
            for h in range(j): clash = clash | (nm[:, :, j] == nm[:, :, h])
            nm[:, :, j] = (nm[:, :, j] + clash) % W
    return nm
def links(rng):
    far = rng.integers(0, W, (8, W, M)); by = np.arange(W)[None, :, None] + rng.integers(-24, 25, (8, W, M))
    return spaced(np.where(rng.random((8, W, M)) < 0.5, far, by))
def among(rng, pool, own):
    keys = np.where(pool[None, :] == own[:, None], 2.0, rng.random((len(own), len(pool))))
    return pool[np.argsort(keys, axis=1)[:, :M]]
def setup_inputs(rng):
    form = rng.integers(0, 16, (8, 16, 24)); kind = rng.integers(0, 24, (8, W))
    x = np.clip(np.stack([form[g][:, kind[g]] for g in range(8)]) + rng.integers(-3, 4, (8, 16, W)), 0, 15)
    m = np.clip(np.add.reduce(x, axis=0) + rng.integers(-40, 41, (16, W)), 0, 120)
    return pack(x, m, links(rng))
def setup_inputs_spread(rng):
    s = 0.5 + 0.5 * rng.random((1, 1, W))
    x = np.floor(16 * s * rng.random((8, 16, W))).astype(np.int64) * (rng.random((1, 1, W)) > 0.0625)
    m = np.floor(121 * (0.6 + 0.4 * rng.random((1, W))) * rng.random((16, W))).astype(np.int64)
    c = np.floor(W * rng.random((8, W, M)) ** 3).astype(np.int64); c[1::2] = W - 1 - c[1::2]
    return pack(x, m, spaced(c))
def setup_inputs_ends(rng):
    one = np.concatenate([np.repeat(np.arange(8), F // 64), np.full(F // 8, 8), np.full(F // 32, 9), np.full(F // 8, 10)])
    one = np.concatenate([one, np.full(F - len(one), 11)])
    kind = np.concatenate([rng.permutation(one) for q in range(N)])
    kind[:60] = np.tile(np.arange(10), 6); kind[W - 60:] = np.tile(np.arange(10), 6)
    edge = np.concatenate([np.arange(60), np.arange(W - 60, W)])
    x = 15 * rng.integers(0, 2, (8, 16, W)); m = 120 * rng.integers(0, 2, (16, W))
    x[:, :, kind < 9] = 0; i = np.flatnonzero(kind < 8); x[kind[i], :, i] = 15
    m[:, kind < 8] = 120; m[:, kind == 8] = 0
    x[:, :, kind == 10] = 15; m[:, kind == 10] = 120 * rng.integers(0, 2, (1, int(np.sum(kind == 10))))
    c = np.where(rng.random((8, W, M)) < 0.5, edge[rng.integers(0, 120, (8, W, M))], rng.integers(0, W, (8, W, M)))
    c[:, :, 0] = 0; c[:, :, M - 1] = W - 1
    nm = spaced(np.take_along_axis(c, np.argsort(rng.random(c.shape), axis=-1), -1))
    full = np.flatnonzero(kind == 10); quiet = edge[kind[edge] == 8]
    for g in range(8):
        loud = edge[kind[edge] == g]
        for who, pool in ((kind == g, loud), ((kind < 9) & (kind != g), quiet), (kind == 9, loud), (kind == 10, full)):
            nm[g, who] = among(rng, pool, np.flatnonzero(who))
    return pack(x, m, nm)
def setup_inputs_corners(rng):
    own = np.arange(W)[:, None]; j = np.arange(M)[None, :]; b = own // (M + 1) * (M + 1)
    ways = [own + 1 + j, own - 1 - j, b + (own - b + 1 + j) % (M + 1), 0 * own + j, 0 * own + W - 1 - j, 0 * own + np.where(j % 2 == 0, j // 2, W - 1 - j // 2),
            np.where(j == 0, own ^ 1, own + W // 2 + 2 * j), own + F * (j + 1)]
    p = rng.permutation(8)
    c = np.stack([np.concatenate([ways[(int(p[g]) + q) % 8][q * F:(q + 1) * F] for q in range(N)]) for g in range(8)])
    z = rng.integers(4, 12, (8, 16, 1)); kind = rng.integers(0, 4, (8, 1, W)); o = np.argsort(rng.random((8, 16, W)), axis=1)
    size = np.where(kind == 0, 0, np.where(kind == 1, 2, np.where(o < np.where(kind == 2, H, H - 1), 1, 3)))
    x = z + size * (2 * rng.integers(0, 2, (8, 16, W)) - 1)
    m = np.clip(np.add.reduce(x, axis=0) + rng.choice(np.array([-24, 0, 24]), (1, W)), 0, 120)
    return pack(x, m, spaced(c))
def setup_inputs_calm(rng):
    x = rng.integers(4, 12, (8, 16, 1)) + rng.integers(0, 2, (8, 16, W))
    m = np.clip(np.add.reduce(x, axis=0) + rng.integers(-3, 4, (16, W)), 0, 120)
    return pack(x, m, links(rng))
def steps(rng, x, m, nm, kind, quiet):
    left = rng.permutation(np.flatnonzero(kind == 33)); h, h2 = [int(g) for g in rng.permutation(8)[:2]]; others = [g for g in range(8) if g != h]
    cut = np.add.accumulate(np.array([M, M, M, M, M + 1, M + 1, 7, 7, 8, 8])); who = left[:int(cut[-1]) + 8 * N]
    p1a, p1b, p2a, p2b, p3a, p3b, da, db, sa, sb, ask = np.split(who, cut)
    x[:, :, who] = 0; m[:, who] = 0
    for g in range(8): nm[g, who] = among(rng, quiet, who)
    m1 = rng.integers(20, 60, 16); m2 = rng.integers(40, 80, (16, 1)); m3 = rng.integers(40, 70, (16, 1))
    up = np.where(rng.permutation(16) < H, 1, rng.integers(-1, 1, 16))
    m[:, p1a] = m1[:, None]; m[:, p1b] = (m1 + up)[:, None]
    md = rng.integers(80, 99, (16, 7)); ms = rng.integers(104, 121, (16, 8))
    for p1, p2, p3, d, s in ((p1a, p2a, p3a, da, sa), (p1b, p2b, p3b, db, sb)):
        m[:, p2] = m2; m[:, p3] = m3; m[:, d] = md; m[:, s] = ms
        nm[h, p2] = among(rng, p1, p2); nm[h2, p3] = among(rng, p2, p3); nm[h, p3] = among(rng, p3, p3)
        nm[h, d] = among(rng, p3, d); nm[h, s] = among(rng, p3, s)
    j = int(rng.integers(0, M)); k = (j + T - 1) % M
    for i, g in enumerate(others):
        two = np.array([da[i], db[i]]); nm[g, two] = among(rng, np.flatnonzero(kind == g + 16), two); nm[g, da[i], k] = db[i]
        for n in range(8):
            two = np.array([sa[n], sb[n]]); nm[g, two] = among(rng, np.flatnonzero(kind == g + 16 * int(rng.integers(0, 2))), two); nm[g, sa[n], k] = sb[n]
        nm[g, ask[::2], j] = da[i]; nm[g, ask[1::2], j] = sa[(np.arange(len(ask[1::2])) + i) % 8]
def setup_inputs_loud(rng):
    one = np.concatenate([np.repeat(np.arange(24), F // 64), np.repeat(np.arange(24, 32), F // 20), np.full(F // 16, 32)])
    one = np.concatenate([one, np.full(F - len(one), 33)])
    kind = np.concatenate([rng.permutation(one) for q in range(N)])
    x = rng.integers(0, 16, (8, 16, W)); x[:, :, kind < 33] = 0
    i = np.flatnonzero(kind < 32); x[kind[i] % 8, :, i] = 15
    m = np.clip(np.add.reduce(x, axis=0) + rng.integers(-40, 41, (16, W)), 0, 120); m[:, kind == 32] = 0
    nm = spaced(rng.integers(0, W, (8, W, M)))
    quiet = rng.permutation(np.flatnonzero(kind == 32))[:64]
    width = rng.permutation(np.array([3, 4, 6, 8, 12, 16, 25, 25]))
    for g in range(8):
        low, mid, high, free = [np.flatnonzero(kind == g + 8 * h) for h in range(4)]
        still = np.flatnonzero((kind == 32) | ((kind < 32) & (kind % 8 != g)))
        nm[g, still] = among(rng, quiet, still)
        nm[g, free] = among(rng, free, free); nm[g, high] = among(rng, high, high); nm[g, low] = among(rng, low, low)
        nm[g, low, np.arange(len(low)) % M] = rng.choice(high, len(low))
        nm[g, mid] = among(rng, high, mid)
        half = np.argsort(rng.random((len(mid), M)), axis=1) < M // 2
        for j in range(M):
            s = mid[half[:, j]]; nm[g, s, j] = rng.choice(low[(j + T - 1) % M::M], len(s))
        c = rng.integers(98, 120, 16); step = 1 + (rng.permutation(16) < H - 1)
        m[:, low] = (c - step)[:, None]; m[:, mid] = c[:, None]; m[:, high] = (c + 1)[:, None]
        w = int(width[g]); m[:, free] = rng.integers(96, 122 - w, (16, 1)) + rng.integers(0, w, (16, len(free)))
    steps(rng, x, m, nm, kind, quiet)
    return pack(x, m, nm)
def check_ranges(d):
    bad = []
    for k, hi in (("x", 15), ("mix", 120), ("nb", W - 1)):
        v = np.asarray(d[k]).astype(np.float64)
        if not np.all((v >= 0) & (v <= hi)): bad.append("range of " + k)
        elif np.any(v != np.floor(v)): bad.append("whole numbers of " + k)
    nm = np.stack([gentries(a) for a in d["nb"]]).astype(np.int64).reshape(N, 8, M, F)
    if np.any(nm == np.arange(W).reshape(N, 1, 1, F)): bad.append("a frame names itself in nb")
    s = np.sort(nm, axis=2)
    if np.any(s[:, :, 1:] == s[:, :, :-1]): bad.append("a frame's names in nb repeat")
    return bad
def reference(x, mix, nb):
    a = np.ascontiguousarray(x.astype(np.float64).reshape(N, 8, 16, F).transpose(1, 2, 0, 3)).reshape(8, 16, W)
    m = np.ascontiguousarray(mix.astype(np.float64).transpose(1, 0, 2)).reshape(16, W)
    nm = np.stack([gentries(b) for b in nb]).astype(np.int64).reshape(N, 8, M, F)
    nm = np.ascontiguousarray(nm.transpose(1, 2, 0, 3)).reshape(8, M, W)
    own = np.arange(W)
    for t in range(T):
        v = np.stack([a[g][:, nm[g]] for g in range(8)])
        e = np.sort(np.concatenate([a[:, :, None], v], axis=2), axis=2)[:, :, M // 2]
        c = np.take_along_axis(np.roll(nm, -(t % M), axis=1), nm, 2)
        void = c == own
        for i in range(M): void = void | (c == nm[:, i:i + 1])
        for j in range(1, M): void[:, j] = void[:, j] | np.any(c[:, :j] == c[:, j:j + 1], axis=1)
        u = np.stack([a[g][:, c[g]] for g in range(8)])
        near = np.abs(u - a[:, :, None]) < np.abs(v - a[:, :, None])
        n = np.add.reduce(near.astype(np.int64), axis=1)
        nm = np.where((n >= H) & ~void, c, nm)
        if t < T - 1: a = np.maximum(e + 0.125 * (m - np.add.reduce(e, axis=0)), 0.0)
    e2 = e * e
    return {"ye": np.ascontiguousarray(e2.reshape(128, N, F).transpose(1, 0, 2)).astype(np.float32),
            "yd": np.ascontiguousarray(np.add.reduce(e2, axis=0).reshape(16, N, F).transpose(1, 0, 2)).astype(np.float32),
            "yn": np.stack([gtable(np.ascontiguousarray(nm[:, :, q * F:(q + 1) * F]).reshape(8, -1)) for q in range(N)]).astype(np.float32)}

def check_inputs(d):
    bad = list(check_ranges(d))
    if not bad:
        for name, y in reference(**d).items():
            for q in range(N):
                v = np.abs(np.asarray(y[q], np.float64)); s = np.sqrt(np.mean(v * v))
                if v.max() > 12 * s or s < 2.0 ** 4: bad.append('%s of rank %d is uneven or too small' % (name, q))
    return bad

@@ -1,0 +1,652 @@
+import numpy as np
+from concourse.bass import DstId, RemoteDMATransfer
+from concourse.mybir import AluOpType, ActivationFunctionType
+
+NR, F, W, ROUNDS = 4, 1024, 4096, 5
+NARROW = (True, True, False, False, False)
+PESUB = [(1, 1), (1, 1), (0, 0), (0, 0), (0, 0)]
+
+SCRATCH = {
+    "xw0": ("sbuf", [128, W], "bfloat16"), "xw1": ("sbuf", [128, W], "bfloat16"),
+    "xw2": ("sbuf", [128, W], "float32"), "xw3": ("sbuf", [128, W], "float32"), "xw4": ("sbuf", [128, W], "float32"),
+    "nw0": ("sbuf", [128, W], "bfloat16"), "nw1": ("sbuf", [128, W], "bfloat16"), "nw2": ("sbuf", [128, W], "bfloat16"),
+    "nw3": ("sbuf", [128, W], "bfloat16"), "nw4": ("sbuf", [128, W], "bfloat16"),
+    "nbi": ("sbuf", [128, 256], "int32"), "nmf": ("sbuf", [128, 448], "float32"),
+    "off": ("sbuf", [128, 256], "uint16"), "cof": ("sbuf", [128, 256], "uint16"),
+    "dig": ("sbuf", [128, 512], "bfloat16"), "own": ("sbuf", [128, 256], "float32"),
+    "csb": ("sbuf", [128, 256], "float32"), "dlt": ("sbuf", [128, 256], "float32"),
+    "eq": ("sbuf", [128, 1408], "bfloat16"), "owd": ("sbuf", [128, 512], "bfloat16"),
+    "ds": ("sbuf", [128, 2048], "float32"), "dp": ("sbuf", [128, 2048], "float32"), "dpb": ("sbuf", [128, 2048], "bfloat16"),
+    "adv": ("sbuf", [128, W], "float32"), "cg": ("sbuf", [128, W], "bfloat16"),
+    "du": ("sbuf", [128, 2048], "float32"), "near": ("sbuf", [128, W], "bfloat16"),
+    "lo": ("sbuf", [128, F], "float32"), "hi": ("sbuf", [128, F], "float32"),
+    "pp": ("sbuf", [128, F], "float32"), "qq": ("sbuf", [128, F], "float32"),
+    "ppb": ("sbuf", [128, F], "bfloat16"), "qqb": ("sbuf", [128, F], "bfloat16"),
+    "xa0": ("sbuf", [128, F], "bfloat16"), "xa1": ("sbuf", [128, F], "bfloat16"), "xa2": ("sbuf", [128, F], "float32"),
+    "xa3": ("sbuf", [128, F], "float32"), "xa4": ("sbuf", [128, F], "float32"),
+    "yes": ("sbuf", [128, F], "float32"), "mixb": ("sbuf", [128, F], "bfloat16"),
+    "un": ("sbuf", [128, 2064], "bfloat16"), "aw": ("sbuf", [128, 720], "bfloat16"), "zz": ("sbuf", [128, 128], "bfloat16"),
+    "ib": ("sbuf", [128, 128], "bfloat16"), "nib": ("sbuf", [128, 128], "bfloat16"), "n16": ("sbuf", [128, 128], "bfloat16"),
+    "mb": ("sbuf", [128, 128], "bfloat16"), "nmb": ("sbuf", [128, 128], "bfloat16"), "e8": ("sbuf", [128, 128], "bfloat16"),
+    "idf": ("sbuf", [128, 128], "float32"), "nidf": ("sbuf", [128, 128], "float32"),
+    "mf": ("sbuf", [128, 128], "float32"), "nmtx": ("sbuf", [128, 128], "float32"),
+    "bm8": ("sbuf", [128, 128], "float32"), "b16": ("sbuf", [128, 16], "float32"),
+    "i1": ("sbuf", [128, 128], "int32"), "i2": ("sbuf", [128, 128], "int32"), "i3": ("sbuf", [128, 128], "int32"),
+    "i4": ("sbuf", [128, 256], "int32"), "i5": ("sbuf", [128, 128], "int32"), "i6": ("sbuf", [128, 128], "int32"),
+    "pc": ("sbuf", [128, 4], "int32"), "pcf": ("sbuf", [128, 4], "float32"),
+    "ps": ("psum", [128, 4096], "float32"),
+}
+SEMAPHORES = (["pe", "dve", "act", "pool", "sent", "lx", "ln", "lm", "oe0", "oe1", "od", "on0", "on1"]
+              + [s % (t, h) for s in ("ax%d_%d", "cx%d_%d") for t in range(ROUNDS) for h in range(2)] + ["an%d" % t for t in range(ROUNDS)])
+
+BANK = 512
+UB = 4 * BANK
+CB = 6 * BANK + 384
+UPE = [(), (), (), (), ()]
+VOIDPE = [0, 0, 0, 0, 0]
+EQ = {0: [0, 256, 512, 768], 1: [64, 320, 576, 832, 1024], 2: [128, 384, 640, 896, 1088, 1216],
+      3: [192, 448, 704, 960, 1152, 1280, 1344]}
+
+
+def A(name, c0, c1, step=1, p0=0, p1=128):
+    return (name, c0, c1, step, p0, p1)
+
+
+def plan(r):
+    ops = []
+
+    def add(eng, kind, args, reads, writes, token=None):
+        rd = []
+        for a in reads:
+            if a[0] == "ind":
+                rd += [a[1], a[2]]
+            else:
+                rd.append(a)
+        ops.append({"eng": eng, "kind": kind, "args": args, "reads": rd, "writes": list(writes), "token": token})
+
+    def tt(out, a, b, op):
+        add("dve", "tt", (out, a, b, op), [a, b], [out])
+
+    def ts(out, a, s1, s2, op0, op1=None):
+        add("dve", "ts", (out, a, s1, s2, op0, op1), [a] + [s for s in (s1, s2) if isinstance(s, tuple)], [out])
+
+    def cp(out, a):
+        add("dve", "cp", (out, a), [a], [out])
+
+    def ms(out, v):
+        add("dve", "ms", (out, v), [], [out])
+
+    def act(out, a, func, scale=1.0, bias=0.0):
+        add("act", "act", (out, a, func, scale, bias), [a], [out])
+
+    def mm(items):
+        add("pe", "mm", items, [i[1] for i in items] + [i[2] for i in items], [i[0] for i in items])
+
+    def iota(out, pattern, base, cm):
+        add("pool", "iota", (out, pattern, base, cm), [], [out])
+
+    def dma(eng, out, a, sem):
+        add(eng, "dma", (out, a, sem), [a], [out], (sem, 16))
+
+    def send(a, sem, to=None):
+        add("pool", "send", (a, sem, to or a), [a], [])
+
+    def arrive(name, c0, c1, sem):
+        add("none", "arr", (sem,), [], [A(name, q * F + c0, q * F + c1) for q in range(NR) if q != r], (sem, None))
+
+    o = r * F
+    cut = TUNE["cut"]
+    SN, PN = TUNE["pairs"]
+    NB = [6 * BANK + 64 * j if j < cut else 7 * BANK + 64 * j for j in range(4)]
+    DB = [c + 192 for c in NB]
+
+    def xo(t, c0=0, c1=F):
+        return A("xa%d" % t, c0, c1)
+
+    def xs(t, c0=0, c1=F):
+        return A("xw%d" % t, o + c0, o + c1)
+
+    def gx(t, lst, j):
+        return ("ind", A("xw%d" % t, 0, W), A(lst, 64 * j, 64 * j + 64))
+
+    def ps(c0, n, step=1, p1=128):
+        return A("ps", c0, c0 + n, step, 0, p1)
+
+    def row_open():
+        mm([(ps(UB + BANK * h, BANK), A("zz", 0, 128), A("un", 0, BANK), True, False) for h in range(2)])
+
+    def row_names(k0, k1, last):
+        it = []
+        for k in range(k0, k1):
+            for d in range(2):
+                for m in range(16):
+                    s = 128 * m + 15 - (2 * k + d)
+                    end = last and k == k1 - 1 and d == 1 and m >= 14
+                    b = UB + BANK * (m % 2)
+                    it.append((A("ps", b + m // 2, b + BANK, 8), A("un", s, s + 128),
+                               A("dig", 256 * d + 64 * k, 256 * d + 64 * k + 64), False, end))
+        mm(it)
+
+    def row_send(t):
+        for h in range(2):
+            act(A("nw%d" % t, o + h, o + F, 2), ps(UB + BANK * h, BANK), "Copy")
+        send(A("nw%d" % t, o, o + F), "an%d" % t)
+        arrive("nw%d" % t, 0, F, "an%d" % t)
+
+    def lists(k0, k1):
+        nm = A("nmf", 64 * k0, 64 * k1)
+        cp(A("off", 64 * k0, 64 * k1), nm)
+        if TUNE["hidve"] and k1 == 4:
+            cp(A("dig", 64 * k0, 64 * k1), nm)
+        else:
+            act(A("dig", 64 * k0, 64 * k1), nm, "Copy")
+
+    def low_digit(k0, k1):
+        tt(A("dig", 256 + 64 * k0, 256 + 64 * k1), A("nmf", 64 * k0, 64 * k1), A("dig", 64 * k0, 64 * k1), "subtract")
+
+    def choose(t, k0, k1):
+        n = ps(NB[k0], 64 * (k1 - k0))
+        nm = A("nmf", 64 * k0, 64 * k1)
+        if VOIDPE[t] & 2:
+            ts(A("dlt", 64 * k0, 64 * k1), n, 8.5, None, "is_ge")
+            tt(n, ps(DB[k0], 64 * (k1 - k0)), A("dlt", 64 * k0, 64 * k1), "mult")
+        else:
+            ts(n, n, 8.5, None, "is_ge")
+            tt(n, n, A("dlt", 64 * k0, 64 * k1), "mult")
+        tt(nm, n, nm, "add")
+
+    def d_vec(t, j, buf, s):
+        tt(A(buf, F * s, F * s + F), gx(t, "off", j), xo(t), "subtract")
+
+    def v_act(t, s):
+        act(A("dpb" if NARROW[t] else "dp", F * s, F * s + F), gx(t, "off", PN[s]), "Copy")
+
+    def d_open(t, s):
+        for h in range(2):
+            mm([(ps(F * s + BANK * h, BANK), A("nib" if NARROW[t] else "nidf", 0, 128), xo(t, BANK * h, BANK * h + BANK), True, False)])
+
+    def d_close(t, s):
+        for h in range(2):
+            c = F * s + BANK * h
+            mm([(ps(c, BANK), A("ib" if NARROW[t] else "idf", 0, 128), A("dpb" if NARROW[t] else "dp", c, c + BANK), False, True)])
+
+    def d_copy(s):
+        for h in range(2):
+            c = F * s + BANK * h
+            act(ps(c, BANK), A("dp", c, c + BANK), "Copy")
+
+    def abs_s(j, buf, s):
+        act(A("adv", F * j, F * j + F), A(buf, F * s, F * s + F), "Abs")
+
+    def abs_p(s):
+        for h in range(2):
+            c = F * PN[s] + BANK * h
+            act(A("adv", c, c + BANK), ps(F * s + BANK * h, BANK), "Abs")
+
+    def H(name, h, base=0):
+        return A(name, base + BANK * h, base + BANK * h + BANK)
+
+    def pair0():
+        for h in range(2):
+            tt(H("lo", h), H("ps", h), H("ds", h), "min")
+        for h in range(2):
+            tt(H("ps", h), H("ps", h), H("ds", h), "max")
+
+    def pair1():
+        for h in range(2):
+            tt(H("hi", h), H("ps", h, F), H("ds", h, F), "max")
+        for h in range(2):
+            tt(H("ps", h, F), H("ps", h, F), H("ds", h, F), "min")
+
+    def middle(h):
+        tt(H("lo", h), H("ps", h, F), H("lo", h), "max")
+        tt(H("ps", h), H("ps", h), H("hi", h), "min")
+
+    def inner(h):
+        tt(H("pp", h), H("ps", h), H("lo", h), "min")
+        tt(H("qq", h), H("ps", h), H("lo", h), "max")
+
+    def z_open(t):
+        for h in range(2):
+            if t == ROUNDS - 1:
+                mm([(H("ps", h, UB), A("idf", 0, 128), xo(t, BANK * h, BANK * h + BANK), True, False)])
+            else:
+                mm([(H("ps", h, UB), A("e8", 0, 128, 1, 0, 16), A("mixb", BANK * h, BANK * h + BANK, 1, 0, 16), True, False),
+                    (H("ps", h, UB), A("mb" if NARROW[t] else "mf", 0, 128), xo(t, BANK * h, BANK * h + BANK), False, False)])
+
+    def clamp(t, h):
+        sfx = "b" if NARROW[t] else ""
+        act(H("pp" + sfx, h), H("pp", h), "Relu")
+        act(H("qq" + sfx, h), H("qq", h), "Relu", -1.0)
+        pos, neg = ("idf", "nidf") if t == ROUNDS - 1 else (("mb", "nmb") if NARROW[t] else ("mf", "nmtx"))
+        mm([(H("ps", h, UB), A(pos, 0, 128), H("pp" + sfx, h), False, False),
+            (H("ps", h, UB), A(neg, 0, 128), H("qq" + sfx, h), False, True)])
+
+    def x_new(t, h):
+        if t < ROUNDS - 1:
+            act(xo(t + 1, BANK * h, BANK * h + BANK), H("ps", h, UB), "Relu")
+            send(xo(t + 1, BANK * h, BANK * h + BANK), "ax%d_%d" % (t + 1, h), xs(t + 1, BANK * h, BANK * h + BANK))
+            dma("sp", xs(t + 1, BANK * h, BANK * h + BANK), xo(t + 1, BANK * h, BANK * h + BANK), "cx%d_%d" % (t + 1, h))
+            arrive("xw%d" % (t + 1), BANK * h, BANK * h + BANK, "ax%d_%d" % (t + 1, h))
+        else:
+            act(H("yes", h), H("ps", h, UB), "Square")
+            dma("sp", H("ye", h), H("yes", h), "oe%d" % h)
+            mm([(ps(UB + BANK * h, BANK, 1, 16), A("b16", 0, 16), H("yes", h), True, True)])
+
+    def sums():
+        for h in range(2):
+            act(A("dp", BANK * h, BANK * h + BANK, 1, 0, 16), ps(UB + BANK * h, BANK, 1, 16), "Copy")
+        dma("sp", A("yd", 0, F, 1, 0, 16), A("dp", 0, F, 1, 0, 16), "od")
+
+    def c_rows(t, j):
+        act(A("cg", F * j, F * j + F), ("ind", A("nw%d" % t, 0, W), A("off", 64 * j, 64 * j + 64)), "Copy")
+        k = (j + t) % 4
+        mm([(ps(CB + 64 * j, 64), A("aw", 144 * k + 15 - m, 144 * k + 143 - m), A("cg", F * j + m, F * j + F, 16), m == 0, m == 15)
+            for m in range(16)])
+
+    def c_list(j0, j1):
+        cp(A("cof", 64 * j0, 64 * j1), ps(CB + 64 * j0, 64 * (j1 - j0)))
+
+    def less(out, j0, j1, k0, src):
+        n = 64 * (j1 - j0)
+        return [(out, A("idf", 0, 128), A("csb", 64 * j0, 64 * j1), True, False),
+                (out, A("nib", 0, 128), A(src, 64 * k0, 64 * k0 + n), False, False),
+                (out, A("nib", 0, 128), A(src, 256 + 64 * k0, 256 + 64 * k0 + n), False, True)]
+
+    def clashes(t):
+        c = ps(CB, 256)
+        if VOIDPE[t] & 1:
+            for h in range(2):
+                b = UB + BANK * h
+                it = []
+                for i in (2 * h, 2 * h + 1):
+                    b = UB + 256 * i
+                    if i == 0:
+                        it += less(ps(b, 256), 0, 4, 0, "owd")
+                    else:
+                        it += less(ps(b, 64 * (4 - i)), 0, 4 - i, i, "dig") + less(ps(b + 64 * (4 - i), 64 * i), 4 - i, 4, 0, "dig")
+                mm(it)
+                act(H("ps", h, UB), H("ps", h, UB), "Abs")
+                act(H("eq", h), H("ps", h, UB), "Relu", -1.0, 1.0)
+        else:
+            tt(A("eq", 0, 256), c, A("own", 0, 256), "is_equal")
+            for i in range(1, 4):
+                tt(A("eq", 256 * i, 256 * i + 256), c, A("nmf", 64 * i, 64 * i + 256), "is_equal")
+        if VOIDPE[t] & 2:
+            mm(less(ps(DB[0], 64 * cut), 0, cut, 0, "dig"))
+            mm(less(ps(DB[cut], 64 * (4 - cut)), cut, 4, cut, "dig"))
+        else:
+            tt(A("dlt", 0, 256), c, A("nmf", 0, 256), "subtract")
+        tt(A("eq", 1024, 1216), ps(CB + 64, 192), A("csb", 0, 192), "is_equal")
+        tt(A("eq", 1216, 1344), ps(CB + 128, 128), A("csb", 0, 128), "is_equal")
+        tt(A("eq", 1344, 1408), ps(CB + 192, 64), A("csb", 0, 64), "is_equal")
+
+    def u_vec(t, j):
+        s = j % 2
+        if j in UPE[t]:
+            d_open(t, s)
+            act(A("dpb" if NARROW[t] else "dp", F * s, F * s + F), gx(t, "cof", j), "Copy")
+            d_close(t, s)
+            for h in range(2):
+                act(H("ps", h, F * s), H("ps", h, F * s), "Abs")
+            return
+        tt(A("du", F * s, F * s + F), gx(t, "cof", j), xo(t), "subtract")
+        for h in range(2):
+            act(H("ps", h, F * s), H("du", h, F * s), "Abs")
+
+    def compare(j):
+        for h in range(2):
+            tt(H("near", h, F * j), H("ps", h, F * (j % 2)), H("adv", h, F * j), "is_lt")
+
+    def count(j):
+        out = ps(NB[j], 64)
+        it = [(out, A("n16", 0, 128), A("eq", c, c + 64), i == 0, False) for i, c in enumerate(EQ[j])]
+        it += [(out, A("aw", 576 + 15 - m, 576 + 143 - m), A("near", F * j + m, F * j + F, 16), False, m == 15) for m in range(16)]
+        mm(it)
+
+    dma("sp", xo(0), A("x", 0, F), "lx")
+    dma("sp", xs(0), A("x", 0, F), "cx0_0")
+    dma("act", A("nbi", 0, 256), A("nb", 0, 256), "ln")
+    dma("sp", A("mixb", 0, F, 1, 0, 16), A("mix", 0, F, 1, 0, 16), "lm")
+    iota(A("i2", 0, 128), [[1, 16], [16, 8]], 0, -1)
+    iota(A("i1", 0, 128), [[-1, 128]], 128, 1)
+    iota(A("i4", 0, 256), [[0, 4], [16, 64]], o, 1)
+    send(xo(0), "ax0_0", xs(0))
+    arrive("xw0", 0, F, "ax0_0")
+    ms(A("un", 0, 2064), 0.0)
+    ms(A("zz", 0, 128), 0.0)
+    ms(A("aw", 0, 720), 0.0)
+    ts(A("un", 15, 2063, 16), A("i2", 0, 128), 0.0, None, "is_equal")
+    ts(A("ib", 0, 128), A("i1", 0, 128), 128.0, None, "is_equal")
+    row_open()
+    cp(A("nmf", 0, 256), A("nbi", 0, 256))
+    act(A("dig", 0, 256), A("nmf", 0, 256), "Copy")
+    cp(A("off", 0, 256), A("nbi", 0, 256))
+    low_digit(0, 4)
+    row_names(0, 4, True)
+    act(A("nib", 0, 128), A("ib", 0, 128), "Copy", -1.0)
+    ts(A("i3", 0, 128), A("i1", 0, 128), 15, None, "bitwise_and")
+    ts(A("i5", 0, 128), A("i1", 0, 128), 1, None, "arith_shift_right")
+    ts(A("i6", 0, 128), A("i1", 0, 128), 4, None, "arith_shift_right")
+    ts(A("pc", 0, 1), A("i1", 0, 1), 112, None, "bitwise_and")
+    ts(A("bm8", 0, 128), A("i3", 0, 128), 0.0, -0.125, "is_equal", "mult")
+    for k in range(4):
+        ts(A("aw", 144 * k + 15, 144 * k + 143, 16), A("i5", 2 * k, 128, 16), 64.0, None, "is_equal")
+    ts(A("aw", 576 + 15, 576 + 143, 16), A("i6", 0, 128, 16), 8.0, None, "is_equal")
+    cp(A("pcf", 0, 1), A("pc", 0, 1))
+    tt(A("mf", 0, 128), A("bm8", 0, 128), A("ib", 0, 128), "add")
+    ts(A("own", 0, 256), A("i4", 0, 256), A("pcf", 0, 1), None, "subtract")
+    if any(v & 1 for v in VOIDPE):
+        cp(A("owd", 0, 256), A("own", 0, 256))
+        tt(A("owd", 256, 512), A("own", 0, 256), A("owd", 0, 256), "subtract")
+    act(A("e8", 0, 128), A("bm8", 0, 128), "Copy", -1.0)
+    act(A("mb", 0, 128), A("mf", 0, 128), "Copy")
+    act(A("nmb", 0, 128), A("mf", 0, 128), "Copy", -1.0)
+    act(A("n16", 0, 128), A("ib", 0, 128), "Copy", -16.0)
+    act(A("nmtx", 0, 128), A("mf", 0, 128), "Copy", -1.0)
+    act(A("idf", 0, 128), A("ib", 0, 128), "Copy")
+    act(A("nidf", 0, 128), A("ib", 0, 128), "Copy", -1.0)
+    act(A("b16", 0, 16), A("bm8", 0, 16), "Copy", -8.0)
+    row_send(0)
+
+    for t in range(ROUNDS):
+        last = t == ROUNDS - 1
+        for s in range(2):
+            d_vec(t, SN[s], "ds", s)
+            abs_s(SN[s], "ds", s)
+            if PESUB[t][s]:
+                d_open(t, s)
+                v_act(t, s)
+                d_close(t, s)
+                abs_p(s)
+            else:
+                d_vec(t, PN[s], "dp", s)
+                d_copy(s)
+                abs_s(PN[s], "dp", s)
+        z_open(t)
+        pair0()
+        pair1()
+        if not VOIDPE[t] & 1:
+            act(A("nmf", 256, 448), A("nmf", 0, 192), "Copy")
+        middle(0)
+        middle(1)
+        c_rows(t, 0)
+        inner(0)
+        c_rows(t, 1)
+        clamp(t, 0)
+        inner(1)
+        if TUNE["single"]:
+            c_list(0, 1)
+            c_list(1, 2)
+        else:
+            c_list(0, 2)
+        clamp(t, 1)
+        x_new(t, 0)
+        x_new(t, 1)
+        c_rows(t, 2)
+        u_vec(t, 0)
+        c_rows(t, 3)
+        n = 256 if VOIDPE[t] else 192
+        act(A("csb", 0, n), ps(CB, n), "Copy")
+        u_vec(t, 1)
+        if last:
+            sums()
+        if TUNE["single"] > 1:
+            c_list(2, 3)
+            c_list(3, 4)
+        else:
+            c_list(2, 4)
+        compare(0)
+        clashes(t)
+        count(0)
+        u_vec(t, 2)
+        compare(1)
+        count(1)
+        if not last:
+            row_open()
+        u_vec(t, 3)
+        compare(2)
+        count(2)
+        compare(3)
+        count(3)
+        for k0, k1 in ((0, cut), (cut, 4)):
+            choose(t, k0, k1)
+            if last:
+                dma("sp", A("yn", 64 * k0, 64 * k1), A("nmf", 64 * k0, 64 * k1), "on%d" % (k0 > 0))
+            else:
+                lists(k0, k1)
+                low_digit(k0, k1)
+                row_names(k0, k1, k1 == 4)
+        if not last:
+            row_send(t + 1)
+    return ops
+
+
+def width(a):
+    return 16 * (a[2][2] - a[2][1]) if a[0] == "ind" else len(range(a[1], a[2], a[3]))
+
+
+def size(a):
+    return 2 if a[0] in SCRATCH and SCRATCH[a[0]][2] in ("bfloat16", "uint16") else 4
+
+
+def span(op):
+    kind, a = op["kind"], op["args"]
+    if kind == "arr":
+        return 0.0, 0.0
+    if kind == "dma":
+        return 0.1, 2.5
+    if kind == "send":
+        return 0.8, 2.5 + width(a[0]) * size(a[0]) * 128 * (NR - 1) / 3e5
+    if kind == "mm":
+        c = 0.06 + sum(max(64, width(i[2])) * (4 if size(i[2]) == 4 else 1) for i in a) * TUNE["pe"]
+        return c, c
+    n = max(64, width(a[0]))
+    if kind == "iota":
+        n = 2 * n + 128
+    elif kind != "ms" and a[1][0] == "ind":
+        n *= TUNE["gather"]
+    elif kind == "tt" and a[1][0] != "ps" and a[2][0] != "ps":
+        n *= 2
+    elif kind != "act" and kind != "tt" and size(a[0]) == 2 and (kind == "ms" or size(a[1]) == 2):
+        n *= 0.5
+    return 0.06 + n * 1.04e-3, 0.06 + n * 1.04e-3
+
+
+TUNE = {"pe": 0.55e-3, "gather": 1.5, "ahead": 0.0, "cut": 3, "single": 0, "hidve": 1, "pairs": ((0, 2), (1, 3))}
+BIAS = {}
+
+
+def label(op):
+    a = (op["writes"] or op["reads"])[0]
+    name = a[0].rstrip("01234")
+    return "%s %s %s %d" % (op["eng"], op["kind"], name, a[1] % F if name in ("xw", "nw") else a[1])
+
+
+ORDER = {"order": [int(v) for v in """
+9 6 2 0 5 3 1 11 13 10 20 4 12 15 16 18 24 14 19 40 17 21 25 31 23 22 32 33 28 30 26 29 37 35 39 74 38 7 8 46 57 58 42 43 44 41 34 55 49 50 52 48 51 66 59 60 70 61 64 54 67 53 27 62 71 72 69 68 76 75 45 83 63 56 84 73 79 80 107 108 78 81 77 88 36 47 102 103 65 90 89 92 104 106 82 105 86 85 110 111 112 91 87 94 93 98 100 96 99 113 116 120 119 114 117 125 115 127 129 118 132 128 109 124 131 121 122 130 95 97 101 126 135 136 137 134 133 138 170 139 171 123 140 141 142 143 145 146 147 144 168 163 169 148 149 150 151 172 152 153 159 154 161 155 156 157 173 183 164 179 174 176 184 166 175 181 162 165 180 189 185 167 187 160 188 186 182 194 190 191 201 195 202 158 192 177 193 196 197 203 217 223 215 220 219 228 198 199 221 216 226 230 231 232 229 218 238 200 178 205 207 209 208 204 225 224 206 211 212 213 242 233 227 241 245 240 222 237 234 243 210 239 235 236 249 248 250 247 252 246 251 214 254 255 256 258 257 253 244 259 260 261 262 263 265 266 278 279 272 273 267 268 284 269 270 285 264 280 282 274 291 276 294 281 275 287 289 283 277 286 298 288 293 290 297 308 292 296 271 303 304 309 295 302 301 299 300 310 330 324 327 328 322 323 338 336 340 305 306 311 331 325 312 333 337 339 334 326 345 307 314 315 329 335 332 352 346 313 318 319 320 347 349 344 348 341 350 342 356 355 357 317 354 353 358 359 343 321 361 362 363 364 360 368 365 366 369 316 379 380 370 385 386 372 373 371 387 351 367 374 375 391 376 392 381 389 398 388 401 397 400 382 399 393 395 383 394 404 396 402 405 415 416 390 384 377 378 406 407 410 403 411 417 434 435 429 430 409 413 408 412 419 431 433 418 437 438 432 440 444 446 443 442 455 447 414 421 422 452 436 449 441 439 420 453 425 454 448 450 445 456 457 424 459 451 458 462 463 464 461 466 460 465 467 468 469 470 472 426 428 475 476 473 477 479 474 471 480 478 481 427 423 492 508 493 486 487 494 488 482 498 483 495 504 506 489 500 502 496 505 497 491 490 510 509 501 516 484 485 517 513 514 518 503 515 507 512 511 523 522 534 499 535 524 536 542 539 540 554 551 548 553 520 519 521 538 537 525 560 543 526 541 527 528 529 555 549 557 550 563 530 544 564 566 556 552 562 570 531 545 561 532 533 546 547 569 565 559 568 573 567 572 558 571 575 576 577 578 574 579 580 581 582
+""".split()]}
+
+
+def needs(ops):
+    if "needs" not in KEPT or len(KEPT["needs"]) != len(ops):
+        before = [set() for op in ops]
+        seen, sends = {}, {}
+        for i, op in enumerate(ops):
+            acc = sorted(set([(a[0], a[1], a[2], False) for a in op["reads"]] + [(a[0], a[1], a[2], True) for a in op["writes"]]))
+            if op["kind"] == "send":
+                sends[op["args"][1]] = i
+            if op["kind"] == "arr":
+                before[i].add(sends[op["args"][0]])
+            for name, c0, c1, w in acc:
+                before[i].update(k for k, d0, d1, dw in seen.get(name, []) if (w or dw) and c0 < d1 and d0 < c1)
+            for name, c0, c1, w in acc:
+                lst = seen.setdefault(name, [])
+                if w:
+                    lst[:] = [e for e in lst if not (c0 <= e[1] and e[2] <= c1)]
+                lst.append((i, c0, c1, w))
+        KEPT["needs"] = before
+    return KEPT["needs"]
+
+
+KEPT = {}
+
+
+def arrange(ops):
+    if "order" not in ORDER:
+        n = len(ops)
+        before = needs(ops)
+        spans = [span(op) for op in ops]
+        after = [[] for op in ops]
+        for i in range(n):
+            for k in before[i]:
+                after[k].append(i)
+        way = [0.0] * n
+        for i in reversed(range(n)):
+            way[i] = spans[i][1] + 0.1 + max([way[k] for k in after[i]] + [0.0])
+        way = [way[i] + BIAS.get(label(ops[i]), 0.0) for i in range(n)]
+        banks = [set(b for a in op["reads"] + op["writes"] if a[0] == "ps" for b in range(a[1] // BANK, (a[2] - 1) // BANK + 1)) for op in ops]
+        left = [len(b) for b in before]
+        ready = [i for i in range(n) if left[i] == 0]
+        stands = [0.0] * n
+        free, held, order = {}, {}, []
+        while ready:
+            start = {}
+            for i in ready:
+                e = ops[i]["eng"]
+                start[i] = max([stands[i], free.get(e, 0.0)] + [held[b][0] + 0.1 for b in banks[i] if b in held and held[b][1] != e])
+            first = min(ready, key=lambda i: (start[i], -way[i]))
+            e = ops[first]["eng"]
+            i = max((k for k in ready if ops[k]["eng"] == e and start[k] <= start[first] + TUNE["ahead"]), key=lambda k: (way[k], -k))
+            ready.remove(i)
+            order.append(i)
+            free[e] = start[i] + spans[i][0]
+            for b in banks[i]:
+                held[b] = (max(start[i] + spans[i][1], held.get(b, (0.0, e))[0]), e)
+            for k in after[i]:
+                stands[k] = max(stands[k], start[i] + spans[i][1] + (0.0 if ops[i]["kind"] in ("send", "arr") else 0.1))
+                left[k] -= 1
+                if left[k] == 0:
+                    ready.append(k)
+        ORDER["order"] = order
+    return [ops[i] for i in ORDER["order"]]
+
+
+def orders(ops):
+    seen = {}
+    for i, op in enumerate(ops):
+        deps = set()
+        acc = [(a, False) for a in op["reads"]] + [(a, True) for a in op["writes"]]
+        acc = sorted(set((a[0], a[1], a[2], w) for a, w in acc))
+        for name, c0, c1, w in acc:
+            for (k, d0, d1, dw) in seen.get(name, []):
+                other = ops[k]["eng"]
+                if name == "ps" and other != op["eng"]:
+                    hit = c0 // BANK <= (d1 - 1) // BANK and d0 // BANK <= (c1 - 1) // BANK
+                elif name == "ps" and other == "pe":
+                    hit = False
+                else:
+                    hit = (w or dw) and c0 < d1 and d0 < c1
+                if hit:
+                    deps.add(k)
+        for name, c0, c1, w in acc:
+            lst = seen.setdefault(name, [])
+            if w and name != "ps":
+                lst[:] = [e for e in lst if not (c0 <= e[1] and e[2] <= c1)]
+            lst.append((i, c0, c1, w))
+            if name == "ps" and len(lst) > 400:
+                del lst[:100]
+        best = {}
+        for k in deps:
+            key = ops[k]["token"][0] if ops[k]["token"] else ops[k]["eng"]
+            if ops[k]["kind"] == "send":
+                continue
+            best[key] = max(best.get(key, -1), k)
+        op["deps"] = best
+    done = {}
+    for i, op in enumerate(ops):
+        have = done.setdefault(op["eng"], {})
+        op["deps"] = {key: k for key, k in op["deps"].items() if have.get(key, -1) < k}
+        have.update(op["deps"])
+    for op in ops:
+        op["signal"] = False
+    for op in ops:
+        if op["kind"] != "arr":
+            for k in op["deps"].values():
+                ops[k]["signal"] = True
+    return ops
+
+
+def rank_program(g, core, T, topo):
+    rank = T.rank_of(core)
+    if rank is None:
+        return
+    peers = [c for c in T.cores if c != core]
+    mask = topo.mask(core, peers[0])
+    for c in peers:
+        mask &= topo.mask(core, c)
+    lanes = len([e for e in topo.engines(core, peers[0]) if mask >> e & 1])
+    dst_ids = [DstId(rid=topo.addr(c)[0], pnc=topo.addr(c)[1]) for c in peers]
+    queue = {"pe": g.tensor, "dve": g.vector, "act": g.scalar, "sp": g.sync, "pool": g}
+    alu = {"add": AluOpType.add, "subtract": AluOpType.subtract, "mult": AluOpType.mult, "max": AluOpType.max,
+           "min": AluOpType.min, "is_ge": AluOpType.is_ge, "is_lt": AluOpType.is_lt, "is_equal": AluOpType.is_equal,
+           "bitwise_and": AluOpType.bitwise_and, "arith_shift_right": AluOpType.arith_shift_right}
+    fun = {"Copy": ActivationFunctionType.Copy, "Abs": ActivationFunctionType.Abs, "Relu": ActivationFunctionType.Relu,
+           "Square": ActivationFunctionType.Square}
+
+    def ap(a):
+        if not isinstance(a, tuple):
+            return a
+        if a[0] == "ind":
+            return ap(a[1]).indirect(ap(a[2]))
+        name, c0, c1, step, p0, p1 = a
+        return T[name][p0:p1, c0:c1] if step == 1 else T[name][p0:p1, c0:c1:step]
+
+    ops = orders(arrange(plan(rank)))
+    count = {"pe": 0, "dve": 0, "act": 0, "pool": 0}
+    sent = 0
+    stores = []
+    for op in ops:
+        kind, a = op["kind"], op["args"]
+        if kind == "arr":
+            op["mark"] = (a[0], lanes * len(peers))
+            continue
+        q = queue[op["eng"]]
+        for k in op["deps"].values():
+            q.wait_ge(T.sem[ops[k]["mark"][0]], ops[k]["mark"][1])
+        if kind == "dma":
+            q.dma_start(ap(a[0]), ap(a[1])).then_inc(T.sem[a[2]], 16)
+            op["mark"] = op["token"]
+            if not op["signal"]:
+                stores.append(a[2])
+            continue
+        if kind == "send":
+            g.remote_dma_fused([RemoteDMATransfer(dst_ids=dst_ids, dma_engine_mask=mask, remote_sem=T.sem[a[1]],
+                                                  src=ap(a[0]), dsts=[ap(a[2]) for c in peers])], local_sem=T.sem.sent)
+            sent += lanes
+            continue
+        if kind == "tt":
+            ins = q.tensor_tensor(ap(a[0]), ap(a[1]), ap(a[2]), alu[a[3]])
+        elif kind == "ts":
+            if a[5] is None:
+                ins = q.tensor_scalar(ap(a[0]), ap(a[1]), ap(a[2]), None, alu[a[4]])
+            else:
+                ins = q.tensor_scalar(ap(a[0]), ap(a[1]), ap(a[2]), ap(a[3]), alu[a[4]], alu[a[5]])
+        elif kind == "cp":
+            ins = q.tensor_copy(ap(a[0]), ap(a[1]))
+        elif kind == "ms":
+            ins = q.memset(ap(a[0]), a[1])
+        elif kind == "act":
+            ins = q.activation(ap(a[0]), ap(a[1]), fun[a[2]], bias=a[4], scale=a[3])
+        elif kind == "iota":
+            ins = q.iota(ap(a[0]), a[1], a[2], a[3])
+        else:
+            for out, lhs, rhs, start, stop in a:
+                ins = q.matmul(ap(out), ap(lhs), ap(rhs), start, stop)
+        if op["signal"]:
+            count[op["eng"]] += 1
+            ins.then_inc(T.sem[op["eng"]], 1)
+            op["mark"] = (op["eng"], count[op["eng"]])
+    for s in stores:
+        g.sync.wait_ge(T.sem[s], 16)
+    g.wait_ge(T.sem.sent, sent)

@@ -1,10 +1,8 @@
-import numpy as np
 from concourse.bass import DstId, RemoteDMATransfer
 from concourse.mybir import AluOpType, ActivationFunctionType
 
 NR, F, W, ROUNDS = 4, 1024, 4096, 5
 NARROW = (True, True, False, False, False)
-PESUB = [(1, 1), (1, 1), (0, 0), (0, 0), (0, 0)]
 
 SCRATCH = {
     "xw0": ("sbuf", [128, W], "bfloat16"), "xw1": ("sbuf", [128, W], "bfloat16"),
@@ -13,47 +11,60 @@ SCRATCH = {
     "nw3": ("sbuf", [128, W], "bfloat16"), "nw4": ("sbuf", [128, W], "bfloat16"),
     "nbi": ("sbuf", [128, 256], "int32"), "nmf": ("sbuf", [128, 448], "float32"),
     "off": ("sbuf", [128, 256], "uint16"), "cof": ("sbuf", [128, 256], "uint16"),
-    "dig": ("sbuf", [128, 512], "bfloat16"), "own": ("sbuf", [128, 256], "float32"),
-    "csb": ("sbuf", [128, 256], "float32"), "dlt": ("sbuf", [128, 256], "float32"),
-    "eq": ("sbuf", [128, 1408], "bfloat16"), "owd": ("sbuf", [128, 512], "bfloat16"),
-    "ds": ("sbuf", [128, 2048], "float32"), "dp": ("sbuf", [128, 2048], "float32"), "dpb": ("sbuf", [128, 2048], "bfloat16"),
+    "dg": ("sbuf", [128, 512], "bfloat16"), "dt": ("sbuf", [128, 16, 2, 16], "bfloat16"), "own": ("sbuf", [128, 256], "float32"),
+    "csb": ("sbuf", [128, 192], "float32"), "dlt": ("sbuf", [128, 256], "float32"), "eq": ("sbuf", [128, 1408], "bfloat16"),
+    "ds": ("sbuf", [128, 2048], "float32"), "dsb": ("sbuf", [128, 2048], "bfloat16"),
+    "dp": ("sbuf", [128, 2048], "float32"), "dpb": ("sbuf", [128, 2048], "bfloat16"),
     "adv": ("sbuf", [128, W], "float32"), "cg": ("sbuf", [128, W], "bfloat16"),
-    "du": ("sbuf", [128, 2048], "float32"), "near": ("sbuf", [128, W], "bfloat16"),
+    "du": ("sbuf", [128, 2048], "float32"), "dub": ("sbuf", [128, 2048], "bfloat16"), "near": ("sbuf", [128, W], "bfloat16"),
     "lo": ("sbuf", [128, F], "float32"), "hi": ("sbuf", [128, F], "float32"),
+    "lob": ("sbuf", [128, F], "bfloat16"), "hib": ("sbuf", [128, F], "bfloat16"),
     "pp": ("sbuf", [128, F], "float32"), "qq": ("sbuf", [128, F], "float32"),
     "ppb": ("sbuf", [128, F], "bfloat16"), "qqb": ("sbuf", [128, F], "bfloat16"),
     "xa0": ("sbuf", [128, F], "bfloat16"), "xa1": ("sbuf", [128, F], "bfloat16"), "xa2": ("sbuf", [128, F], "float32"),
     "xa3": ("sbuf", [128, F], "float32"), "xa4": ("sbuf", [128, F], "float32"),
-    "yes": ("sbuf", [128, F], "float32"), "mixb": ("sbuf", [128, F], "bfloat16"),
-    "un": ("sbuf", [128, 2064], "bfloat16"), "aw": ("sbuf", [128, 720], "bfloat16"), "zz": ("sbuf", [128, 128], "bfloat16"),
+    "mixb": ("sbuf", [128, F], "bfloat16"), "yds": ("sbuf", [128, 128], "float32"),
+    "rs": ("sbuf", [128, 576], "bfloat16"), "aw": ("sbuf", [128, 864], "bfloat16"), "mh": ("sbuf", [128, 64], "bfloat16"),
     "ib": ("sbuf", [128, 128], "bfloat16"), "nib": ("sbuf", [128, 128], "bfloat16"), "n16": ("sbuf", [128, 128], "bfloat16"),
+    "hb": ("sbuf", [128, 128], "bfloat16"),
     "mb": ("sbuf", [128, 128], "bfloat16"), "nmb": ("sbuf", [128, 128], "bfloat16"), "e8": ("sbuf", [128, 128], "bfloat16"),
     "idf": ("sbuf", [128, 128], "float32"), "nidf": ("sbuf", [128, 128], "float32"),
     "mf": ("sbuf", [128, 128], "float32"), "nmtx": ("sbuf", [128, 128], "float32"),
-    "bm8": ("sbuf", [128, 128], "float32"), "b16": ("sbuf", [128, 16], "float32"),
-    "i1": ("sbuf", [128, 128], "int32"), "i2": ("sbuf", [128, 128], "int32"), "i3": ("sbuf", [128, 128], "int32"),
+    "bm8": ("sbuf", [128, 128], "float32"), "bb": ("sbuf", [128, 136], "float32"),
+    "i1": ("sbuf", [128, 144], "int32"), "i3": ("sbuf", [128, 128], "int32"),
     "i4": ("sbuf", [128, 256], "int32"), "i5": ("sbuf", [128, 128], "int32"), "i6": ("sbuf", [128, 128], "int32"),
-    "pc": ("sbuf", [128, 4], "int32"), "pcf": ("sbuf", [128, 4], "float32"),
-    "ps": ("psum", [128, 4096], "float32"),
+    "pc": ("sbuf", [128, 8], "int32"), "pcf": ("sbuf", [128, 8], "float32"),
+    "pa": ("psum", [128, 2048], "float32"), "pu": ("psum", [128, 16, 4, 16], "float32"), "pl": ("psum", [128, 1024], "float32"),
 }
 SEMAPHORES = (["pe", "dve", "act", "pool", "sent", "lx", "ln", "lm", "oe0", "oe1", "od", "on0", "on1"]
-              + [s % (t, h) for s in ("ax%d_%d", "cx%d_%d") for t in range(ROUNDS) for h in range(2)] + ["an%d" % t for t in range(ROUNDS)])
+              + [s % (t, h) for s in ("ax%d_%d", "cx%d_%d", "an%d_%d", "ga%d_%d") for t in range(ROUNDS) for h in range(2)])
 
 BANK = 512
 UB = 4 * BANK
 CB = 6 * BANK + 384
-UPE = [(), (), (), (), ()]
-VOIDPE = [0, 0, 0, 0, 0]
 EQ = {0: [0, 256, 512, 768], 1: [64, 320, 576, 832, 1024], 2: [128, 384, 640, 896, 1088, 1216],
       3: [192, 448, 704, 960, 1152, 1280, 1344]}
 
+OPT = {
+    "cut": 3, "sn": (2, 3), "pn": (0, 1),
+    "pesub": [(1, 1), (1, 1), (1, 2), (1, 2), (1, 2)],
+    "comp1": (0, 0, 0, 0, 0), "comp3": (0, 0, 0, 0, 0),
+    "prod": [(0, 1), (0, 1), (), (), ()], "upe": [(3,), (3,), (), (), ()], "udma": [(), (), (3,), (3,), (3,)],
+    "sign": (), "cof": ((0, 1), (1, 2), (2, 4)),
+    "stage": [(0, F, UB, UB)] * ROUNDS,
+    "whole": ("lo1", "hi1", "hi2", "lo2", "ap", "dc", "ns", "L", "H", "lt0", "lt1"),
+}
 
-def A(name, c0, c1, step=1, p0=0, p1=128):
-    return (name, c0, c1, step, p0, p1)
+
+def A(name, c0, c1, step=1, p0=0, p1=128, idx=None, n=None):
+    return (name, c0, c1, step, p0, p1, idx, n)
 
 
 def plan(r):
-    ops = []
+    ops, now = [], [None, None]
+
+    def at(t, tag):
+        now[0], now[1] = t, tag
 
     def add(eng, kind, args, reads, writes, token=None):
         rd = []
@@ -62,7 +73,7 @@ def plan(r):
                 rd += [a[1], a[2]]
             else:
                 rd.append(a)
-        ops.append({"eng": eng, "kind": kind, "args": args, "reads": rd, "writes": list(writes), "token": token})
+        ops.append({"eng": eng, "kind": kind, "args": args, "reads": rd, "writes": list(writes), "token": token, "tag": tuple(now)})
 
     def tt(out, a, b, op):
         add("dve", "tt", (out, a, b, op), [a, b], [out])
@@ -80,7 +91,7 @@ def plan(r):
         add("act", "act", (out, a, func, scale, bias), [a], [out])
 
     def mm(items):
-        add("pe", "mm", items, [i[1] for i in items] + [i[2] for i in items], [i[0] for i in items])
+        add("pe", "mm", items, [i[1] for i in items] + [i[2] for i in items] + [i[0] for i in items if not i[3]], [i[0] for i in items])
 
     def iota(out, pattern, base, cm):
         add("pool", "iota", (out, pattern, base, cm), [], [out])
@@ -95,465 +106,372 @@ def plan(r):
         add("none", "arr", (sem,), [], [A(name, q * F + c0, q * F + c1) for q in range(NR) if q != r], (sem, None))
 
     o = r * F
-    cut = TUNE["cut"]
-    SN, PN = TUNE["pairs"]
+    cut, SN, PN = OPT["cut"], OPT["sn"], OPT["pn"]
     NB = [6 * BANK + 64 * j if j < cut else 7 * BANK + 64 * j for j in range(4)]
-    DB = [c + 192 for c in NB]
 
-    def xo(t, c0=0, c1=F):
-        return A("xa%d" % t, c0, c1)
+    def H(name, h, base=0):
+        return A(name, base, base + F) if h is None else A(name, base + BANK * h, base + BANK * h + BANK)
 
-    def xs(t, c0=0, c1=F):
-        return A("xw%d" % t, o + c0, o + c1)
+    def parts(t, tag, s=""):
+        for h in ([None] if tag in OPT["whole"] or tag + str(s) in OPT["whole"] else [0, 1]):
+            at(t, tag + str(s) + ("" if h is None else "ab"[h]))
+            yield h
+
+    def halves(t, tag, s=""):
+        for h in range(2):
+            at(t, tag + str(s) + "ab"[h])
+            yield h
+
+    def xo(t, h=None):
+        return H("xa%d" % t, h)
+
+    def xs(t, h=None):
+        return H("xw%d" % t, h, o)
 
     def gx(t, lst, j):
         return ("ind", A("xw%d" % t, 0, W), A(lst, 64 * j, 64 * j + 64))
 
-    def ps(c0, n, step=1, p1=128):
-        return A("ps", c0, c0 + n, step, 0, p1)
+    def ps(c0, n):
+        return A("ps", c0, c0 + n)
 
-    def row_open():
-        mm([(ps(UB + BANK * h, BANK), A("zz", 0, 128), A("un", 0, BANK), True, False) for h in range(2)])
+    def M(name):
+        return A(name, 0, 128)
 
-    def row_names(k0, k1, last):
-        it = []
-        for k in range(k0, k1):
-            for d in range(2):
-                for m in range(16):
-                    s = 128 * m + 15 - (2 * k + d)
-                    end = last and k == k1 - 1 and d == 1 and m >= 14
-                    b = UB + BANK * (m % 2)
-                    it.append((A("ps", b + m // 2, b + BANK, 8), A("un", s, s + 128),
-                               A("dig", 256 * d + 64 * k, 256 * d + 64 * k + 64), False, end))
-        mm(it)
+    def group(out, terms, start=True):
+        return [(out, M(m) if isinstance(m, str) else m, a, start and i == 0, i == len(terms) - 1) for i, (m, a) in enumerate(terms)]
 
-    def row_send(t):
-        for h in range(2):
-            act(A("nw%d" % t, o + h, o + F, 2), ps(UB + BANK * h, BANK), "Copy")
-        send(A("nw%d" % t, o, o + F), "an%d" % t)
-        arrive("nw%d" % t, 0, F, "an%d" % t)
-
-    def lists(k0, k1):
-        nm = A("nmf", 64 * k0, 64 * k1)
-        cp(A("off", 64 * k0, 64 * k1), nm)
-        if TUNE["hidve"] and k1 == 4:
-            cp(A("dig", 64 * k0, 64 * k1), nm)
+    def digits(t, k):
+        nm, hi = A("nmf", 64 * k, 64 * k + 64), A("dg", 2 * k, 512, 8)
+        at(t, "dh%d" % k)
+        if k == 3:
+            cp(hi, nm)
         else:
-            act(A("dig", 64 * k0, 64 * k1), nm, "Copy")
+            act(hi, nm, "Copy")
+        at(t, "dl%d" % k)
+        tt(A("dg", 2 * k + 1, 512, 8), nm, hi, "subtract")
 
-    def low_digit(k0, k1):
-        tt(A("dig", 256 + 64 * k0, 256 + 64 * k1), A("nmf", 64 * k0, 64 * k1), A("dig", 64 * k0, 64 * k1), "subtract")
+    def rows(t, u):
+        at(t, "turn")
+        add("dve", "tr", (A("dt", 0, 512, idx=(slice(0, 128),)), A("dg", 0, 512)), [A("dg", 0, 512)], [A("dt", 0, 512)])
+        for h in halves(t, "row"):
+            blk = slice(8 * h, 8 * h + 8)
+            it = []
+            for c2 in range(4):
+                out = A("ps", UB + BANK * h, UB + BANK * h + BANK, idx=(slice(0, 128), blk, c2), n=128)
+                it += group(out, [(A("rs", 144 * c2 + 16 * (1 - g0), 144 * c2 + 16 * (1 - g0) + 128),
+                                   A("dt", 256 * h, 256 * h + 256, idx=(slice(0, 128), blk, g0), n=128)) for g0 in range(2)])
+            mm(it)
+        for h in parts(t, "rc"):
+            act(H("nw%d" % u, h, o), H("ps", h, UB), "Copy")
+        for h in parts(t, "ns"):
+            a = H("nw%d" % u, h, o)
+            send(a, "an%d_%d" % (u, h or 0))
+            arrive("nw%d" % u, a[1] - o, a[2] - o, "an%d_%d" % (u, h or 0))
 
-    def choose(t, k0, k1):
-        n = ps(NB[k0], 64 * (k1 - k0))
-        nm = A("nmf", 64 * k0, 64 * k1)
-        if VOIDPE[t] & 2:
-            ts(A("dlt", 64 * k0, 64 * k1), n, 8.5, None, "is_ge")
-            tt(n, ps(DB[k0], 64 * (k1 - k0)), A("dlt", 64 * k0, 64 * k1), "mult")
-        else:
-            ts(n, n, 8.5, None, "is_ge")
-            tt(n, n, A("dlt", 64 * k0, 64 * k1), "mult")
-        tt(nm, n, nm, "add")
+    def one(tag):
+        at(-1, tag)
 
-    def d_vec(t, j, buf, s):
-        tt(A(buf, F * s, F * s + F), gx(t, "off", j), xo(t), "subtract")
-
-    def v_act(t, s):
-        act(A("dpb" if NARROW[t] else "dp", F * s, F * s + F), gx(t, "off", PN[s]), "Copy")
-
-    def d_open(t, s):
-        for h in range(2):
-            mm([(ps(F * s + BANK * h, BANK), A("nib" if NARROW[t] else "nidf", 0, 128), xo(t, BANK * h, BANK * h + BANK), True, False)])
-
-    def d_close(t, s):
-        for h in range(2):
-            c = F * s + BANK * h
-            mm([(ps(c, BANK), A("ib" if NARROW[t] else "idf", 0, 128), A("dpb" if NARROW[t] else "dp", c, c + BANK), False, True)])
-
-    def d_copy(s):
-        for h in range(2):
-            c = F * s + BANK * h
-            act(ps(c, BANK), A("dp", c, c + BANK), "Copy")
-
-    def abs_s(j, buf, s):
-        act(A("adv", F * j, F * j + F), A(buf, F * s, F * s + F), "Abs")
-
-    def abs_p(s):
-        for h in range(2):
-            c = F * PN[s] + BANK * h
-            act(A("adv", c, c + BANK), ps(F * s + BANK * h, BANK), "Abs")
-
-    def H(name, h, base=0):
-        return A(name, base + BANK * h, base + BANK * h + BANK)
-
-    def pair0():
-        for h in range(2):
-            tt(H("lo", h), H("ps", h), H("ds", h), "min")
-        for h in range(2):
-            tt(H("ps", h), H("ps", h), H("ds", h), "max")
-
-    def pair1():
-        for h in range(2):
-            tt(H("hi", h), H("ps", h, F), H("ds", h, F), "max")
-        for h in range(2):
-            tt(H("ps", h, F), H("ps", h, F), H("ds", h, F), "min")
-
-    def middle(h):
-        tt(H("lo", h), H("ps", h, F), H("lo", h), "max")
-        tt(H("ps", h), H("ps", h), H("hi", h), "min")
-
-    def inner(h):
-        tt(H("pp", h), H("ps", h), H("lo", h), "min")
-        tt(H("qq", h), H("ps", h), H("lo", h), "max")
-
-    def z_open(t):
-        for h in range(2):
-            if t == ROUNDS - 1:
-                mm([(H("ps", h, UB), A("idf", 0, 128), xo(t, BANK * h, BANK * h + BANK), True, False)])
-            else:
-                mm([(H("ps", h, UB), A("e8", 0, 128, 1, 0, 16), A("mixb", BANK * h, BANK * h + BANK, 1, 0, 16), True, False),
-                    (H("ps", h, UB), A("mb" if NARROW[t] else "mf", 0, 128), xo(t, BANK * h, BANK * h + BANK), False, False)])
-
-    def clamp(t, h):
-        sfx = "b" if NARROW[t] else ""
-        act(H("pp" + sfx, h), H("pp", h), "Relu")
-        act(H("qq" + sfx, h), H("qq", h), "Relu", -1.0)
-        pos, neg = ("idf", "nidf") if t == ROUNDS - 1 else (("mb", "nmb") if NARROW[t] else ("mf", "nmtx"))
-        mm([(H("ps", h, UB), A(pos, 0, 128), H("pp" + sfx, h), False, False),
-            (H("ps", h, UB), A(neg, 0, 128), H("qq" + sfx, h), False, True)])
-
-    def x_new(t, h):
-        if t < ROUNDS - 1:
-            act(xo(t + 1, BANK * h, BANK * h + BANK), H("ps", h, UB), "Relu")
-            send(xo(t + 1, BANK * h, BANK * h + BANK), "ax%d_%d" % (t + 1, h), xs(t + 1, BANK * h, BANK * h + BANK))
-            dma("sp", xs(t + 1, BANK * h, BANK * h + BANK), xo(t + 1, BANK * h, BANK * h + BANK), "cx%d_%d" % (t + 1, h))
-            arrive("xw%d" % (t + 1), BANK * h, BANK * h + BANK, "ax%d_%d" % (t + 1, h))
-        else:
-            act(H("yes", h), H("ps", h, UB), "Square")
-            dma("sp", H("ye", h), H("yes", h), "oe%d" % h)
-            mm([(ps(UB + BANK * h, BANK, 1, 16), A("b16", 0, 16), H("yes", h), True, True)])
-
-    def sums():
-        for h in range(2):
-            act(A("dp", BANK * h, BANK * h + BANK, 1, 0, 16), ps(UB + BANK * h, BANK, 1, 16), "Copy")
-        dma("sp", A("yd", 0, F, 1, 0, 16), A("dp", 0, F, 1, 0, 16), "od")
-
-    def c_rows(t, j):
-        act(A("cg", F * j, F * j + F), ("ind", A("nw%d" % t, 0, W), A("off", 64 * j, 64 * j + 64)), "Copy")
-        k = (j + t) % 4
-        mm([(ps(CB + 64 * j, 64), A("aw", 144 * k + 15 - m, 144 * k + 143 - m), A("cg", F * j + m, F * j + F, 16), m == 0, m == 15)
-            for m in range(16)])
-
-    def c_list(j0, j1):
-        cp(A("cof", 64 * j0, 64 * j1), ps(CB + 64 * j0, 64 * (j1 - j0)))
-
-    def less(out, j0, j1, k0, src):
-        n = 64 * (j1 - j0)
-        return [(out, A("idf", 0, 128), A("csb", 64 * j0, 64 * j1), True, False),
-                (out, A("nib", 0, 128), A(src, 64 * k0, 64 * k0 + n), False, False),
-                (out, A("nib", 0, 128), A(src, 256 + 64 * k0, 256 + 64 * k0 + n), False, True)]
-
-    def clashes(t):
-        c = ps(CB, 256)
-        if VOIDPE[t] & 1:
-            for h in range(2):
-                b = UB + BANK * h
-                it = []
-                for i in (2 * h, 2 * h + 1):
-                    b = UB + 256 * i
-                    if i == 0:
-                        it += less(ps(b, 256), 0, 4, 0, "owd")
-                    else:
-                        it += less(ps(b, 64 * (4 - i)), 0, 4 - i, i, "dig") + less(ps(b + 64 * (4 - i), 64 * i), 4 - i, 4, 0, "dig")
-                mm(it)
-                act(H("ps", h, UB), H("ps", h, UB), "Abs")
-                act(H("eq", h), H("ps", h, UB), "Relu", -1.0, 1.0)
-        else:
-            tt(A("eq", 0, 256), c, A("own", 0, 256), "is_equal")
-            for i in range(1, 4):
-                tt(A("eq", 256 * i, 256 * i + 256), c, A("nmf", 64 * i, 64 * i + 256), "is_equal")
-        if VOIDPE[t] & 2:
-            mm(less(ps(DB[0], 64 * cut), 0, cut, 0, "dig"))
-            mm(less(ps(DB[cut], 64 * (4 - cut)), cut, 4, cut, "dig"))
-        else:
-            tt(A("dlt", 0, 256), c, A("nmf", 0, 256), "subtract")
-        tt(A("eq", 1024, 1216), ps(CB + 64, 192), A("csb", 0, 192), "is_equal")
-        tt(A("eq", 1216, 1344), ps(CB + 128, 128), A("csb", 0, 128), "is_equal")
-        tt(A("eq", 1344, 1408), ps(CB + 192, 64), A("csb", 0, 64), "is_equal")
-
-    def u_vec(t, j):
-        s = j % 2
-        if j in UPE[t]:
-            d_open(t, s)
-            act(A("dpb" if NARROW[t] else "dp", F * s, F * s + F), gx(t, "cof", j), "Copy")
-            d_close(t, s)
-            for h in range(2):
-                act(H("ps", h, F * s), H("ps", h, F * s), "Abs")
-            return
-        tt(A("du", F * s, F * s + F), gx(t, "cof", j), xo(t), "subtract")
-        for h in range(2):
-            act(H("ps", h, F * s), H("du", h, F * s), "Abs")
-
-    def compare(j):
-        for h in range(2):
-            tt(H("near", h, F * j), H("ps", h, F * (j % 2)), H("adv", h, F * j), "is_lt")
-
-    def count(j):
-        out = ps(NB[j], 64)
-        it = [(out, A("n16", 0, 128), A("eq", c, c + 64), i == 0, False) for i, c in enumerate(EQ[j])]
-        it += [(out, A("aw", 576 + 15 - m, 576 + 143 - m), A("near", F * j + m, F * j + F, 16), False, m == 15) for m in range(16)]
-        mm(it)
-
+    one("load")
     dma("sp", xo(0), A("x", 0, F), "lx")
-    dma("sp", xs(0), A("x", 0, F), "cx0_0")
     dma("act", A("nbi", 0, 256), A("nb", 0, 256), "ln")
+    dma("sp", xs(0), A("x", 0, F), "cx0_0")
     dma("sp", A("mixb", 0, F, 1, 0, 16), A("mix", 0, F, 1, 0, 16), "lm")
-    iota(A("i2", 0, 128), [[1, 16], [16, 8]], 0, -1)
-    iota(A("i1", 0, 128), [[-1, 128]], 128, 1)
+    iota(A("i1", 0, 144), [[-1, 144]], 128, 1)
     iota(A("i4", 0, 256), [[0, 4], [16, 64]], o, 1)
     send(xo(0), "ax0_0", xs(0))
     arrive("xw0", 0, F, "ax0_0")
-    ms(A("un", 0, 2064), 0.0)
-    ms(A("zz", 0, 128), 0.0)
-    ms(A("aw", 0, 720), 0.0)
-    ts(A("un", 15, 2063, 16), A("i2", 0, 128), 0.0, None, "is_equal")
-    ts(A("ib", 0, 128), A("i1", 0, 128), 128.0, None, "is_equal")
-    row_open()
+    ms(A("aw", 0, 864), 0.0)
+    ms(A("bb", 0, 136), 0.0)
+    ts(A("pc", 4, 8), A("i1", 0, 32, 8), 31, 3, "bitwise_and", "arith_shift_right")
+    ts(M("ib"), M("i1"), 128.0, None, "is_equal")
+    ts(A("pcf", 4, 8), A("pc", 4, 8), 0.0, None, "is_equal")
+    ts(M("i3"), M("i1"), 15, None, "bitwise_and")
+    for c2 in range(4):
+        ts(A("rs", 144 * c2, 144 * c2 + 144), A("i1", 0, 144), 112.0 + 8 * c2, A("pcf", 4 + c2, 5 + c2), "is_equal", "mult")
+    act(M("nib"), M("ib"), "Copy", -1.0)
+    act(M("hb"), M("ib"), "Copy", 0.5)
+    one("list")
     cp(A("nmf", 0, 256), A("nbi", 0, 256))
-    act(A("dig", 0, 256), A("nmf", 0, 256), "Copy")
+    one("off")
     cp(A("off", 0, 256), A("nbi", 0, 256))
-    low_digit(0, 4)
-    row_names(0, 4, True)
-    act(A("nib", 0, 128), A("ib", 0, 128), "Copy", -1.0)
-    ts(A("i3", 0, 128), A("i1", 0, 128), 15, None, "bitwise_and")
-    ts(A("i5", 0, 128), A("i1", 0, 128), 1, None, "arith_shift_right")
-    ts(A("i6", 0, 128), A("i1", 0, 128), 4, None, "arith_shift_right")
+    for k in range(4):
+        digits(-1, k)
+    rows(-1, 0)
+    one("more")
+    ts(M("i5"), M("i1"), 1, None, "arith_shift_right")
+    ts(M("i6"), M("i1"), 4, None, "arith_shift_right")
     ts(A("pc", 0, 1), A("i1", 0, 1), 112, None, "bitwise_and")
-    ts(A("bm8", 0, 128), A("i3", 0, 128), 0.0, -0.125, "is_equal", "mult")
+    ts(M("bm8"), M("i3"), 0.0, -0.125, "is_equal", "mult")
     for k in range(4):
         ts(A("aw", 144 * k + 15, 144 * k + 143, 16), A("i5", 2 * k, 128, 16), 64.0, None, "is_equal")
     ts(A("aw", 576 + 15, 576 + 143, 16), A("i6", 0, 128, 16), 8.0, None, "is_equal")
+    ts(A("aw", 720 + 15, 720 + 143, 16), A("i6", 0, 128, 16), 8.0, 0.5, "is_equal", "mult")
+    ms(A("mh", 0, 64), -0.5)
     cp(A("pcf", 0, 1), A("pc", 0, 1))
-    tt(A("mf", 0, 128), A("bm8", 0, 128), A("ib", 0, 128), "add")
+    tt(M("mf"), M("bm8"), M("ib"), "add")
     ts(A("own", 0, 256), A("i4", 0, 256), A("pcf", 0, 1), None, "subtract")
-    if any(v & 1 for v in VOIDPE):
-        cp(A("owd", 0, 256), A("own", 0, 256))
-        tt(A("owd", 256, 512), A("own", 0, 256), A("owd", 0, 256), "subtract")
-    act(A("e8", 0, 128), A("bm8", 0, 128), "Copy", -1.0)
-    act(A("mb", 0, 128), A("mf", 0, 128), "Copy")
-    act(A("nmb", 0, 128), A("mf", 0, 128), "Copy", -1.0)
-    act(A("n16", 0, 128), A("ib", 0, 128), "Copy", -16.0)
-    act(A("nmtx", 0, 128), A("mf", 0, 128), "Copy", -1.0)
-    act(A("idf", 0, 128), A("ib", 0, 128), "Copy")
-    act(A("nidf", 0, 128), A("ib", 0, 128), "Copy", -1.0)
-    act(A("b16", 0, 16), A("bm8", 0, 16), "Copy", -8.0)
-    row_send(0)
+    one("mats")
+    act(M("e8"), M("bm8"), "Copy", -1.0)
+    act(M("n16"), M("ib"), "Copy", -16.0)
+    act(M("idf"), M("ib"), "Copy")
+    act(M("nidf"), M("ib"), "Copy", -1.0)
+    act(A("bb", 7, 135, 8), A("bm8", 0, 16), "Copy", -8.0)
+    act(M("mb"), M("mf"), "Copy")
+    act(M("nmb"), M("mf"), "Copy", -1.0)
+    act(M("nmtx"), M("mf"), "Copy", -1.0)
+
+    def d_open(t, u):
+        for s in range(2):
+            if OPT["pesub"][u][s] == 1:
+                for h in halves(t, "do", s):
+                    mm([(H("ps", h, F * s), M("nib" if NARROW[u] else "nidf"), xo(u, h), True, False)])
+
+    d_open(-1, 0)
 
     for t in range(ROUNDS):
         last = t == ROUNDS - 1
+        b = "b" if NARROW[t] else ""
+        pos, neg = ("ib", "nib") if NARROW[t] else ("idf", "nidf")
+        prod, upe, stage = OPT["prod"][t], OPT["upe"][t], OPT["stage"][t]
+        P = [lambda h: H("ps", h), lambda h: H("ps", h, F)]
+
         for s in range(2):
-            d_vec(t, SN[s], "ds", s)
-            abs_s(SN[s], "ds", s)
-            if PESUB[t][s]:
-                d_open(t, s)
-                v_act(t, s)
-                d_close(t, s)
-                abs_p(s)
+            at(t, "d%d" % s)
+            tt(H("ds" + b, None, F * s), gx(t, "off", SN[s]), xo(t), "subtract")
+            at(t, "as%d" % s)
+            act(H("adv", None, F * SN[s]), H("ds" + b, None, F * s), "Abs")
+            at(t, "v%d" % s)
+            if OPT["pesub"][t][s] == 2:
+                tt(H("dp", None, F * s), gx(t, "off", PN[s]), xo(t), "subtract")
+                for h in halves(t, "dx", s):
+                    mm([(P[s](h), M(pos), H("dp", h, F * s), True, True)])
+            elif OPT["pesub"][t][s]:
+                act(H("dp" + b, None, F * s), gx(t, "off", PN[s]), "Copy")
+                for h in halves(t, "dx", s):
+                    mm([(P[s](h), M(pos), H("dp" + b, h, F * s), False, True)])
             else:
-                d_vec(t, PN[s], "dp", s)
-                d_copy(s)
-                abs_s(PN[s], "dp", s)
-        z_open(t)
-        pair0()
-        pair1()
-        if not VOIDPE[t] & 1:
-            act(A("nmf", 256, 448), A("nmf", 0, 192), "Copy")
-        middle(0)
-        middle(1)
-        c_rows(t, 0)
-        inner(0)
-        c_rows(t, 1)
-        clamp(t, 0)
-        inner(1)
-        if TUNE["single"]:
-            c_list(0, 1)
-            c_list(1, 2)
-        else:
-            c_list(0, 2)
-        clamp(t, 1)
-        x_new(t, 0)
-        x_new(t, 1)
-        c_rows(t, 2)
-        u_vec(t, 0)
-        c_rows(t, 3)
-        n = 256 if VOIDPE[t] else 192
-        act(A("csb", 0, n), ps(CB, n), "Copy")
-        u_vec(t, 1)
-        if last:
-            sums()
-        if TUNE["single"] > 1:
-            c_list(2, 3)
-            c_list(3, 4)
-        else:
-            c_list(2, 4)
-        compare(0)
-        clashes(t)
-        count(0)
-        u_vec(t, 2)
-        compare(1)
-        count(1)
-        if not last:
-            row_open()
-        u_vec(t, 3)
-        compare(2)
-        count(2)
-        compare(3)
-        count(3)
-        for k0, k1 in ((0, cut), (cut, 4)):
-            choose(t, k0, k1)
+                tt(H("dp", None, F * s), gx(t, "off", PN[s]), xo(t), "subtract")
+                for h in parts(t, "dc", s):
+                    act(P[s](h), H("dp", h, F * s), "Copy")
+            if PN[s] not in prod:
+                for h in parts(t, "ap", s):
+                    act(H("adv", h, F * PN[s]), P[s](h), "Abs")
+        at(t, "ext")
+        act(A("nmf", 256, 448), A("nmf", 0, 192), "Copy")
+
+        for h in halves(t, "zo"):
             if last:
-                dma("sp", A("yn", 64 * k0, 64 * k1), A("nmf", 64 * k0, 64 * k1), "on%d" % (k0 > 0))
+                mm([(H("ps", h, UB), M("idf"), xo(t, h), True, False)])
             else:
-                lists(k0, k1)
-                low_digit(k0, k1)
-                row_names(k0, k1, k1 == 4)
+                mm([(H("ps", h, UB), A("e8", 0, 128, 1, 0, 16), A("mixb", BANK * h, BANK * h + BANK, 1, 0, 16), True, False),
+                    (H("ps", h, UB), M("mb" if b else "mf"), xo(t, h), False, False)])
+        for h in parts(t, "lo1"):
+            tt(H("lo" + b, h), P[0](h), H("ds" + b, h), "min")
+        for h in parts(t, "hi2"):
+            tt(H("hi" + b, h), P[1](h), H("ds" + b, h, F), "max")
+        if OPT["comp1"][t]:
+            for h in halves(t, "hi1"):
+                mm(group(P[0](h), [(pos, H("dp" + b, h)), (neg, xo(t, h)), (pos, H("ds" + b, h)), (neg, H("lo" + b, h))]))
+            for h in halves(t, "lo2"):
+                mm(group(P[1](h), [(pos, H("dp" + b, h, F)), (neg, xo(t, h)), (pos, H("ds" + b, h, F)), (neg, H("hi" + b, h))]))
+        else:
+            for h in parts(t, "hi1"):
+                tt(P[0](h), P[0](h), H("ds" + b, h), "max")
+            for h in parts(t, "lo2"):
+                tt(P[1](h), P[1](h), H("ds" + b, h, F), "min")
+        for h in parts(t, "L"):
+            tt(H("lo" + b, h), P[1](h), H("lo" + b, h), "max")
+        for h in parts(t, "H"):
+            tt(H("hi" + b, h) if OPT["comp3"][t] else P[0](h), P[0](h), H("hi" + b, h), "min")
+        if OPT["comp3"][t]:
+            for h in halves(t, "lh"):
+                mm(group(P[1](h), [(pos, H("lo" + b, h)), (neg, H("hi" + b, h))]))
+            for h in parts(t, "r"):
+                act(H("ds" + b, h), P[1](h), "Relu")
+            for h in halves(t, "p"):
+                mm(group(P[0](h), [(pos, H("lo" + b, h)), (neg, H("ds" + b, h))]))
+            for h in halves(t, "q"):
+                mm(group(P[1](h), [(neg, H("hi" + b, h)), (neg, H("ds" + b, h))]))
+            for h in parts(t, "rp"):
+                act(H("pp" + b, h), P[0](h), "Relu")
+            for h in parts(t, "rq"):
+                act(H("qq" + b, h), P[1](h), "Relu")
+        else:
+            for h in parts(t, "p"):
+                tt(H("pp", h), P[0](h), H("lo" + b, h), "min")
+            for h in parts(t, "q"):
+                tt(H("qq", h), P[0](h), H("lo" + b, h), "max")
+            for h in parts(t, "rp"):
+                act(H("pp" + b, h), H("pp", h), "Relu")
+            for h in parts(t, "rq"):
+                act(H("qq" + b, h), H("qq", h), "Relu", -1.0)
+        zp, zn = ("idf", "nidf") if last else (("mb", "nmb") if b else ("mf", "nmtx"))
+        for h in halves(t, "zc"):
+            mm(group(H("ps", h, UB), [(zp, H("pp" + b, h)), (zn, H("qq" + b, h))], False))
+        for h in halves(t, "xn"):
+            if last:
+                act(H("hi", h), H("ps", h, UB), "Square")
+                dma("sp", H("ye", h), H("hi", h), "oe%d" % h)
+            else:
+                act(xo(t + 1, h), H("ps", h, UB), "Relu")
+                send(xo(t + 1, h), "ax%d_%d" % (t + 1, h), xs(t + 1, h))
+                dma("sp", xs(t + 1, h), xo(t + 1, h), "cx%d_%d" % (t + 1, h))
+                arrive("xw%d" % (t + 1), BANK * h, BANK * h + BANK, "ax%d_%d" % (t + 1, h))
+
+        for j in range(4):
+            at(t, "c%d" % j)
+            act(H("cg", None, F * j), ("ind", A("nw%d" % t, 0, W), A("off", 64 * j, 64 * j + 64)), "Copy")
+            at(t, "cl%d" % j)
+            k = (j + t) % 4
+            mm(group(ps(CB + 64 * j, 64), [(A("aw", 144 * k + 15 - m, 144 * k + 143 - m), A("cg", F * j + m, F * j + F, 16)) for m in range(16)]))
+        for j, j1 in OPT["cof"]:
+            at(t, "cof%d" % j)
+            cp(A("cof", 64 * j, 64 * j1), ps(CB + 64 * j, 64 * (j1 - j)))
+        at(t, "csb")
+        act(A("csb", 0, 192), ps(CB, 192), "Copy")
+        c = ps(CB, 256)
+        for i in range(4):
+            at(t, "e%d" % i)
+            tt(A("eq", 256 * i, 256 * i + 256), c, A("nmf", 64 * i, 64 * i + 256) if i else A("own", 0, 256), "is_equal")
+        at(t, "dlt")
+        tt(A("dlt", 0, 256), c, A("nmf", 0, 256), "subtract")
+        for i, e in ((1, 1024), (2, 1216), (3, 1344)):
+            at(t, "f%d" % i)
+            n = 256 - 64 * i
+            tt(A("eq", e, e + n), ps(CB + 64 * i, n), A("csb", 0, n), "is_equal")
+        for j in range(4):
+            s, base = j % 2, stage[j]
+            if j in prod:
+                v = F * PN.index(j)
+                at(t, "u%d" % j)
+                tt(H("dub", None, F * s), gx(t, "cof", j), H("dpb", None, v), "subtract")
+                for h in halves(t, "uo", j):
+                    mm([(H("ps", h, base), M("ib"), H("dpb", h, v), True, False), (H("ps", h, base), M("nib"), xo(t, h), False, False)])
+                for h in halves(t, "ux", j):
+                    mm([(H("ps", h, base), M("hb"), H("dub", h, F * s), False, True)])
+                for h in parts(t, "lt", j):
+                    tt(H("near", h, F * j), H("ps", h, base), H("dub", h, F * s), "mult")
+                at(t, "neg%d" % j)
+                if j in OPT["sign"]:
+                    act(H("near", None, F * j), H("near", None, F * j), "Sign", -1.0, -1.0 / 256)
+                else:
+                    ts(H("near", None, F * j), H("near", None, F * j), 0.0, None, "is_lt")
+            else:
+                at(t, "u%d" % j)
+                if j in upe:
+                    act(H("ds" + b, None, F * s), gx(t, "cof", j), "Copy")
+                    for h in halves(t, "uo", j):
+                        mm([(H("ps", h, base), M(neg), xo(t, h), True, False)])
+                    for h in halves(t, "ux", j):
+                        mm([(H("ps", h, base), M(pos), H("ds" + b, h, F * s), False, True)])
+                    for h in parts(t, "au", j):
+                        act(H("ps", h, base), H("ps", h, base), "Abs")
+                elif j in OPT["udma"][t]:
+                    u, sem = H("dp", None, F * s), "ga%d_%d" % (t, s)
+                    act(u, gx(t, "cof", j), "Copy", -1.0)
+                    at(t, "ux%d" % j)
+                    add("pool", "gdma", (u, xo(t), sem), [u, xo(t)], [u], (sem, 16))
+                    for h in parts(t, "au", j):
+                        act(H("ps", h, base), H("dp", h, F * s), "Abs")
+                else:
+                    tt(H("du", None, F * s), gx(t, "cof", j), xo(t), "subtract")
+                    for h in parts(t, "au", j):
+                        act(H("ps", h, base), H("du", h, F * s), "Abs")
+                for h in parts(t, "lt", j):
+                    tt(H("near", h, F * j), H("ps", h, base), H("adv", h, F * j), "is_lt")
+            at(t, "n%d" % j)
+            signs = j in prod and j in OPT["sign"]
+            w = 720 if signs else 576
+            mm(group(ps(NB[j], 64), [("n16", A("eq", e, e + 64)) for e in EQ[j]] + [("n16", A("mh", 0, 64))] * signs
+                     + [(A("aw", w + 15 - m, w + 143 - m), A("near", F * j + m, F * j + F, 16)) for m in range(16)]))
+        if last:
+            at(t, "sum")
+            mm(group(ps(BANK, 128), [(A("bb", 7 - i, 135 - i), A("hi", 128 * i, 128 * i + 128)) for i in range(8)]))
+            at(t, "yd")
+            act(M("yds"), ps(BANK, 128), "Copy")
+            dma("sp", A("yd", 0, F, 1, 0, 16), M("yds"), "od")
+        else:
+            d_open(t, t + 1)
+        for k0, k1 in ((0, cut), (cut, 4)):
+            n, nm = ps(NB[k0], 64 * (k1 - k0)), A("nmf", 64 * k0, 64 * k1)
+            at(t, "ge%d" % k0)
+            ts(n, n, 8.5, None, "is_ge")
+            at(t, "mul%d" % k0)
+            tt(n, n, A("dlt", 64 * k0, 64 * k1), "mult")
+            at(t, "new%d" % k0)
+            tt(nm, n, nm, "add")
+            at(t, "off%d" % k0)
+            if last:
+                dma("sp", A("yn", 64 * k0, 64 * k1), nm, "on%d" % (k0 > 0))
+            else:
+                cp(A("off", 64 * k0, 64 * k1), nm)
+                for k in range(k0, k1):
+                    digits(t, k)
         if not last:
-            row_send(t + 1)
+            rows(t, t + 1)
     return ops
 
 
 def width(a):
-    return 16 * (a[2][2] - a[2][1]) if a[0] == "ind" else len(range(a[1], a[2], a[3]))
+    if a[0] == "ind":
+        return 16 * (a[2][2] - a[2][1])
+    return a[7] or len(range(a[1], a[2], a[3]))
 
 
 def size(a):
     return 2 if a[0] in SCRATCH and SCRATCH[a[0]][2] in ("bfloat16", "uint16") else 4
 
 
-def span(op):
-    kind, a = op["kind"], op["args"]
-    if kind == "arr":
-        return 0.0, 0.0
-    if kind == "dma":
-        return 0.1, 2.5
-    if kind == "send":
-        return 0.8, 2.5 + width(a[0]) * size(a[0]) * 128 * (NR - 1) / 3e5
-    if kind == "mm":
-        c = 0.06 + sum(max(64, width(i[2])) * (4 if size(i[2]) == 4 else 1) for i in a) * TUNE["pe"]
-        return c, c
-    n = max(64, width(a[0]))
-    if kind == "iota":
-        n = 2 * n + 128
-    elif kind != "ms" and a[1][0] == "ind":
-        n *= TUNE["gather"]
-    elif kind == "tt" and a[1][0] != "ps" and a[2][0] != "ps":
-        n *= 2
-    elif kind != "act" and kind != "tt" and size(a[0]) == 2 and (kind == "ms" or size(a[1]) == 2):
-        n *= 0.5
-    return 0.06 + n * 1.04e-3, 0.06 + n * 1.04e-3
-
-
-TUNE = {"pe": 0.55e-3, "gather": 1.5, "ahead": 0.0, "cut": 3, "single": 0, "hidve": 1, "pairs": ((0, 2), (1, 3))}
-BIAS = {}
-
-
-def label(op):
-    a = (op["writes"] or op["reads"])[0]
-    name = a[0].rstrip("01234")
-    return "%s %s %s %d" % (op["eng"], op["kind"], name, a[1] % F if name in ("xw", "nw") else a[1])
-
-
-ORDER = {"order": [int(v) for v in """
-9 6 2 0 5 3 1 11 13 10 20 4 12 15 16 18 24 14 19 40 17 21 25 31 23 22 32 33 28 30 26 29 37 35 39 74 38 7 8 46 57 58 42 43 44 41 34 55 49 50 52 48 51 66 59 60 70 61 64 54 67 53 27 62 71 72 69 68 76 75 45 83 63 56 84 73 79 80 107 108 78 81 77 88 36 47 102 103 65 90 89 92 104 106 82 105 86 85 110 111 112 91 87 94 93 98 100 96 99 113 116 120 119 114 117 125 115 127 129 118 132 128 109 124 131 121 122 130 95 97 101 126 135 136 137 134 133 138 170 139 171 123 140 141 142 143 145 146 147 144 168 163 169 148 149 150 151 172 152 153 159 154 161 155 156 157 173 183 164 179 174 176 184 166 175 181 162 165 180 189 185 167 187 160 188 186 182 194 190 191 201 195 202 158 192 177 193 196 197 203 217 223 215 220 219 228 198 199 221 216 226 230 231 232 229 218 238 200 178 205 207 209 208 204 225 224 206 211 212 213 242 233 227 241 245 240 222 237 234 243 210 239 235 236 249 248 250 247 252 246 251 214 254 255 256 258 257 253 244 259 260 261 262 263 265 266 278 279 272 273 267 268 284 269 270 285 264 280 282 274 291 276 294 281 275 287 289 283 277 286 298 288 293 290 297 308 292 296 271 303 304 309 295 302 301 299 300 310 330 324 327 328 322 323 338 336 340 305 306 311 331 325 312 333 337 339 334 326 345 307 314 315 329 335 332 352 346 313 318 319 320 347 349 344 348 341 350 342 356 355 357 317 354 353 358 359 343 321 361 362 363 364 360 368 365 366 369 316 379 380 370 385 386 372 373 371 387 351 367 374 375 391 376 392 381 389 398 388 401 397 400 382 399 393 395 383 394 404 396 402 405 415 416 390 384 377 378 406 407 410 403 411 417 434 435 429 430 409 413 408 412 419 431 433 418 437 438 432 440 444 446 443 442 455 447 414 421 422 452 436 449 441 439 420 453 425 454 448 450 445 456 457 424 459 451 458 462 463 464 461 466 460 465 467 468 469 470 472 426 428 475 476 473 477 479 474 471 480 478 481 427 423 492 508 493 486 487 494 488 482 498 483 495 504 506 489 500 502 496 505 497 491 490 510 509 501 516 484 485 517 513 514 518 503 515 507 512 511 523 522 534 499 535 524 536 542 539 540 554 551 548 553 520 519 521 538 537 525 560 543 526 541 527 528 529 555 549 557 550 563 530 544 564 566 556 552 562 570 531 545 561 532 533 546 547 569 565 559 568 573 567 572 558 571 575 576 577 578 574 579 580 581 582
-""".split()]}
-
-
-def needs(ops):
-    if "needs" not in KEPT or len(KEPT["needs"]) != len(ops):
-        before = [set() for op in ops]
-        seen, sends = {}, {}
-        for i, op in enumerate(ops):
-            acc = sorted(set([(a[0], a[1], a[2], False) for a in op["reads"]] + [(a[0], a[1], a[2], True) for a in op["writes"]]))
-            if op["kind"] == "send":
-                sends[op["args"][1]] = i
-            if op["kind"] == "arr":
-                before[i].add(sends[op["args"][0]])
-            for name, c0, c1, w in acc:
-                before[i].update(k for k, d0, d1, dw in seen.get(name, []) if (w or dw) and c0 < d1 and d0 < c1)
-            for name, c0, c1, w in acc:
-                lst = seen.setdefault(name, [])
-                if w:
-                    lst[:] = [e for e in lst if not (c0 <= e[1] and e[2] <= c1)]
-                lst.append((i, c0, c1, w))
-        KEPT["needs"] = before
-    return KEPT["needs"]
-
-
-KEPT = {}
+ORDER = {
+    "start": "load list do1b dh2 dh1 dh3 dh0 dl1 dl0 dl3 dl2 turn off more do0a rowb rowa do1a rcb rca do0b ns mats",
+    "narrow": "zoa v0 v1 d0 d1 as1 as0 c1 dx0a dx0b c0 dx1a lo1 dx1b zob hi2 hi1 lo2 cl1 H L cof1 cl0 uo1a c2 cl2 c3 qa pa rpa rqa u1 pb cof0 qb cl3 rpb rqb ux1a zca xna zcb u0 cof2 dlt uo1b uo0b u2 csb ext xnb au2a e1 uo0a ux0b ux1b au2b ux0a e2 e3 f1 lt2a lt2b u3 f2 uo3a ux3a lt1 uo3b ux3b e0 n2 neg1 lt0 n1 f3 au3b au3a neg0 n0 lt3a lt3b ge0 mul0 new0 n3 dh1 dh0 dh2 do1a do1b do0b do0a ge3 off0 mul3 dl1 v0+ new3 dl0 dh3 dl2 dl3 turn rowa rowb rca off3 rcb ns",
+    "wide": "dx0a ext d0 v1 dx0b as0 d1 ap0 dx1b dx1a as1 lo1 ap1 hi1 c0 zob c2 c3 cl0 zoa hi2 lo2 H L cof0 c1 pb cl2 rpb qb cl3 pa rqb cof2 u3 cl1 u0 cof1 qa e2 u1 e0 e1 ux3 dlt e3 rpa rqa au0a au0b zcb xnb lt0 zca u2 au1b csb au1a n0 lt1 xna au2b au2a f1 lt2b lt2a f3 do0b sum au3b f2 lt3b au3a n1 n2 lt3a ge0 mul0 new0 yd dh1 dh0 n3 ge3 do0a off0 v0 mul3 dh2 dl1 new3 dl2 dh3 v0+ dl0 dl3 turn rowa rca rowb rcb off3 ns",
+}
 
 
 def arrange(ops):
-    if "order" not in ORDER:
-        n = len(ops)
-        before = needs(ops)
-        spans = [span(op) for op in ops]
-        after = [[] for op in ops]
-        for i in range(n):
-            for k in before[i]:
-                after[k].append(i)
-        way = [0.0] * n
-        for i in reversed(range(n)):
-            way[i] = spans[i][1] + 0.1 + max([way[k] for k in after[i]] + [0.0])
-        way = [way[i] + BIAS.get(label(ops[i]), 0.0) for i in range(n)]
-        banks = [set(b for a in op["reads"] + op["writes"] if a[0] == "ps" for b in range(a[1] // BANK, (a[2] - 1) // BANK + 1)) for op in ops]
-        left = [len(b) for b in before]
-        ready = [i for i in range(n) if left[i] == 0]
-        stands = [0.0] * n
-        free, held, order = {}, {}, []
-        while ready:
-            start = {}
-            for i in ready:
-                e = ops[i]["eng"]
-                start[i] = max([stands[i], free.get(e, 0.0)] + [held[b][0] + 0.1 for b in banks[i] if b in held and held[b][1] != e])
-            first = min(ready, key=lambda i: (start[i], -way[i]))
-            e = ops[first]["eng"]
-            i = max((k for k in ready if ops[k]["eng"] == e and start[k] <= start[first] + TUNE["ahead"]), key=lambda k: (way[k], -k))
-            ready.remove(i)
-            order.append(i)
-            free[e] = start[i] + spans[i][0]
-            for b in banks[i]:
-                held[b] = (max(start[i] + spans[i][1], held.get(b, (0.0, e))[0]), e)
-            for k in after[i]:
-                stands[k] = max(stands[k], start[i] + spans[i][1] + (0.0 if ops[i]["kind"] in ("send", "arr") else 0.1))
-                left[k] -= 1
-                if left[k] == 0:
-                    ready.append(k)
-        ORDER["order"] = order
-    return [ops[i] for i in ORDER["order"]]
+    if not ORDER:
+        return ops
+    steps = {}
+    for op in ops:
+        steps.setdefault(op["tag"], []).append(op)
+    out = []
+    for t in range(-1, ROUNDS):
+        for name in ORDER["start" if t < 0 else "narrow" if NARROW[t] else "wide"].split():
+            out += steps.pop((t + 1, name[:-1]) if name[-1] == "+" else (t, name), [])
+    assert not steps
+    return out
+
+
+def meet(a, b):
+    return a[0] < b[1] and b[0] < a[1] and not (a[2] == b[2] > 1 and (a[0] - b[0]) % a[2])
+
+
+def touches(op):
+    return sorted(set([(a[0], a[1:4], False) for a in op["reads"]] + [(a[0], a[1:4], True) for a in op["writes"]]))
 
 
 def orders(ops):
     seen = {}
     for i, op in enumerate(ops):
         deps = set()
-        acc = [(a, False) for a in op["reads"]] + [(a, True) for a in op["writes"]]
-        acc = sorted(set((a[0], a[1], a[2], w) for a, w in acc))
-        for name, c0, c1, w in acc:
-            for (k, d0, d1, dw) in seen.get(name, []):
+        acc = touches(op)
+        for name, c, w in acc:
+            for k, d, dw in seen.get(name, []):
                 other = ops[k]["eng"]
                 if name == "ps" and other != op["eng"]:
-                    hit = c0 // BANK <= (d1 - 1) // BANK and d0 // BANK <= (c1 - 1) // BANK
+                    hit = c[0] // BANK <= (d[1] - 1) // BANK and d[0] // BANK <= (c[1] - 1) // BANK
                 elif name == "ps" and other == "pe":
                     hit = False
                 else:
-                    hit = (w or dw) and c0 < d1 and d0 < c1
+                    hit = (w or dw) and meet(c, d)
                 if hit:
                     deps.add(k)
-        for name, c0, c1, w in acc:
+        for name, c, w in acc:
             lst = seen.setdefault(name, [])
             if w and name != "ps":
-                lst[:] = [e for e in lst if not (c0 <= e[1] and e[2] <= c1)]
-            lst.append((i, c0, c1, w))
+                lst[:] = [e for e in lst if not (c[0] <= e[1][0] and e[1][1] <= c[1] and (c[2] == 1 or (c[2] == e[1][2] and c[0] == e[1][0])))]
+            lst.append((i, c, w))
             if name == "ps" and len(lst) > 400:
                 del lst[:100]
         best = {}
@@ -592,14 +510,20 @@ def rank_program(g, core, T, topo):
            "min": AluOpType.min, "is_ge": AluOpType.is_ge, "is_lt": AluOpType.is_lt, "is_equal": AluOpType.is_equal,
            "bitwise_and": AluOpType.bitwise_and, "arith_shift_right": AluOpType.arith_shift_right}
     fun = {"Copy": ActivationFunctionType.Copy, "Abs": ActivationFunctionType.Abs, "Relu": ActivationFunctionType.Relu,
-           "Square": ActivationFunctionType.Square}
+           "Square": ActivationFunctionType.Square, "Sign": ActivationFunctionType.Sign}
 
     def ap(a):
         if not isinstance(a, tuple):
             return a
         if a[0] == "ind":
             return ap(a[1]).indirect(ap(a[2]))
-        name, c0, c1, step, p0, p1 = a
+        name, c0, c1, step, p0, p1, idx, n = a
+        if name == "ps":
+            if UB <= c0 < UB + F:
+                return T.pu[idx] if idx else T.pu[p0:p1, (c0 - UB) // 64:(c1 - UB) // 64]
+            name, c0, c1 = ("pa", c0, c1) if c0 < UB else ("pl", c0 - UB - F, c1 - UB - F)
+        if idx:
+            return T[name][idx]
         return T[name][p0:p1, c0:c1] if step == 1 else T[name][p0:p1, c0:c1:step]
 
     ops = orders(arrange(plan(rank)))
@@ -620,6 +544,10 @@ def rank_program(g, core, T, topo):
             if not op["signal"]:
                 stores.append(a[2])
             continue
+        if kind == "gdma":
+            g.dma_start(ap(a[0]), ap(a[1]), accum_op=AluOpType.add).then_inc(T.sem[a[2]], 16)
+            op["mark"] = op["token"]
+            continue
         if kind == "send":
             g.remote_dma_fused([RemoteDMATransfer(dst_ids=dst_ids, dma_engine_mask=mask, remote_sem=T.sem[a[1]],
                                                   src=ap(a[0]), dsts=[ap(a[2]) for c in peers])], local_sem=T.sem.sent)
@@ -634,6 +562,8 @@ def rank_program(g, core, T, topo):
                 ins = q.tensor_scalar(ap(a[0]), ap(a[1]), ap(a[2]), ap(a[3]), alu[a[4]], alu[a[5]])
         elif kind == "cp":
             ins = q.tensor_copy(ap(a[0]), ap(a[1]))
+        elif kind == "tr":
+            ins = q.transpose(ap(a[0]), ap(a[1]))
         elif kind == "ms":
             ins = q.memset(ap(a[0]), a[1])
         elif kind == "act":

from concourse.bass import DstId, RemoteDMATransfer
from concourse.mybir import AluOpType, ActivationFunctionType

NR, F, W, ROUNDS = 4, 1024, 4096, 5
NARROW = (True, True, False, False, False)

SCRATCH = {
    "xw0": ("sbuf", [128, W], "bfloat16"), "xw1": ("sbuf", [128, W], "bfloat16"),
    "xw2": ("sbuf", [128, W], "float32"), "xw3": ("sbuf", [128, W], "float32"), "xw4": ("sbuf", [128, W], "float32"),
    "nw0": ("sbuf", [128, W], "bfloat16"), "nw1": ("sbuf", [128, W], "bfloat16"), "nw2": ("sbuf", [128, W], "bfloat16"),
    "nw3": ("sbuf", [128, W], "bfloat16"), "nw4": ("sbuf", [128, W], "bfloat16"),
    "nbi": ("sbuf", [128, 256], "int32"), "nmf": ("sbuf", [128, 448], "float32"),
    "off": ("sbuf", [128, 256], "uint16"), "cof": ("sbuf", [128, 256], "uint16"),
    "dg": ("sbuf", [128, 512], "bfloat16"), "dt": ("sbuf", [128, 16, 2, 16], "bfloat16"), "own": ("sbuf", [128, 256], "float32"),
    "csb": ("sbuf", [128, 192], "float32"), "dlt": ("sbuf", [128, 256], "float32"), "eq": ("sbuf", [128, 1408], "bfloat16"),
    "ds": ("sbuf", [128, 2048], "float32"), "dsb": ("sbuf", [128, 2048], "bfloat16"),
    "dp": ("sbuf", [128, 2048], "float32"), "dpb": ("sbuf", [128, 2048], "bfloat16"),
    "adv": ("sbuf", [128, W], "float32"), "cg": ("sbuf", [128, W], "bfloat16"),
    "du": ("sbuf", [128, 2048], "float32"), "dub": ("sbuf", [128, 2048], "bfloat16"), "near": ("sbuf", [128, W], "bfloat16"),
    "lo": ("sbuf", [128, F], "float32"), "hi": ("sbuf", [128, F], "float32"),
    "lob": ("sbuf", [128, F], "bfloat16"), "hib": ("sbuf", [128, F], "bfloat16"),
    "pp": ("sbuf", [128, F], "float32"), "qq": ("sbuf", [128, F], "float32"),
    "ppb": ("sbuf", [128, F], "bfloat16"), "qqb": ("sbuf", [128, F], "bfloat16"),
    "xa0": ("sbuf", [128, F], "bfloat16"), "xa1": ("sbuf", [128, F], "bfloat16"), "xa2": ("sbuf", [128, F], "float32"),
    "xa3": ("sbuf", [128, F], "float32"), "xa4": ("sbuf", [128, F], "float32"),
    "mixb": ("sbuf", [128, F], "bfloat16"), "yds": ("sbuf", [128, 128], "float32"),
    "rs": ("sbuf", [128, 576], "bfloat16"), "aw": ("sbuf", [128, 864], "bfloat16"), "mh": ("sbuf", [128, 64], "bfloat16"),
    "ib": ("sbuf", [128, 128], "bfloat16"), "nib": ("sbuf", [128, 128], "bfloat16"), "n16": ("sbuf", [128, 128], "bfloat16"),
    "hb": ("sbuf", [128, 128], "bfloat16"),
    "mb": ("sbuf", [128, 128], "bfloat16"), "nmb": ("sbuf", [128, 128], "bfloat16"), "e8": ("sbuf", [128, 128], "bfloat16"),
    "idf": ("sbuf", [128, 128], "float32"), "nidf": ("sbuf", [128, 128], "float32"),
    "mf": ("sbuf", [128, 128], "float32"), "nmtx": ("sbuf", [128, 128], "float32"),
    "bm8": ("sbuf", [128, 128], "float32"), "bb": ("sbuf", [128, 136], "float32"),
    "i1": ("sbuf", [128, 144], "int32"), "i3": ("sbuf", [128, 128], "int32"),
    "i4": ("sbuf", [128, 256], "int32"), "i5": ("sbuf", [128, 128], "int32"), "i6": ("sbuf", [128, 128], "int32"),
    "pc": ("sbuf", [128, 8], "int32"), "pcf": ("sbuf", [128, 8], "float32"),
    "pa": ("psum", [128, 2048], "float32"), "pu": ("psum", [128, 16, 4, 16], "float32"), "pl": ("psum", [128, 1024], "float32"),
}
SEMAPHORES = (["pe", "dve", "act", "pool", "sent", "lx", "ln", "lm", "oe0", "oe1", "od", "on0", "on1"]
              + [s % (t, h) for s in ("ax%d_%d", "cx%d_%d", "an%d_%d", "ga%d_%d") for t in range(ROUNDS) for h in range(2)])

BANK = 512
UB = 4 * BANK
CB = 6 * BANK + 384
EQ = {0: [0, 256, 512, 768], 1: [64, 320, 576, 832, 1024], 2: [128, 384, 640, 896, 1088, 1216],
      3: [192, 448, 704, 960, 1152, 1280, 1344]}

OPT = {
    "cut": 3, "sn": (2, 3), "pn": (0, 1),
    "pesub": [(1, 1), (1, 1), (1, 2), (1, 2), (1, 2)],
    "comp1": (0, 0, 0, 0, 0), "comp3": (0, 0, 0, 0, 0),
    "prod": [(0, 1), (0, 1), (), (), ()], "upe": [(3,), (3,), (), (), ()], "udma": [(), (), (3,), (3,), (3,)],
    "sign": (), "cof": ((0, 1), (1, 2), (2, 4)),
    "stage": [(0, F, UB, UB)] * ROUNDS,
    "whole": ("lo1", "hi1", "hi2", "lo2", "ap", "dc", "ns", "L", "H", "lt0", "lt1"),
}


def A(name, c0, c1, step=1, p0=0, p1=128, idx=None, n=None):
    return (name, c0, c1, step, p0, p1, idx, n)


def plan(r):
    ops, now = [], [None, None]

    def at(t, tag):
        now[0], now[1] = t, tag

    def add(eng, kind, args, reads, writes, token=None):
        rd = []
        for a in reads:
            if a[0] == "ind":
                rd += [a[1], a[2]]
            else:
                rd.append(a)
        ops.append({"eng": eng, "kind": kind, "args": args, "reads": rd, "writes": list(writes), "token": token, "tag": tuple(now)})

    def tt(out, a, b, op):
        add("dve", "tt", (out, a, b, op), [a, b], [out])

    def ts(out, a, s1, s2, op0, op1=None):
        add("dve", "ts", (out, a, s1, s2, op0, op1), [a] + [s for s in (s1, s2) if isinstance(s, tuple)], [out])

    def cp(out, a):
        add("dve", "cp", (out, a), [a], [out])

    def ms(out, v):
        add("dve", "ms", (out, v), [], [out])

    def act(out, a, func, scale=1.0, bias=0.0):
        add("act", "act", (out, a, func, scale, bias), [a], [out])

    def mm(items):
        add("pe", "mm", items, [i[1] for i in items] + [i[2] for i in items] + [i[0] for i in items if not i[3]], [i[0] for i in items])

    def iota(out, pattern, base, cm):
        add("pool", "iota", (out, pattern, base, cm), [], [out])

    def dma(eng, out, a, sem):
        add(eng, "dma", (out, a, sem), [a], [out], (sem, 16))

    def send(a, sem, to=None):
        add("pool", "send", (a, sem, to or a), [a], [])

    def arrive(name, c0, c1, sem):
        add("none", "arr", (sem,), [], [A(name, q * F + c0, q * F + c1) for q in range(NR) if q != r], (sem, None))

    o = r * F
    cut, SN, PN = OPT["cut"], OPT["sn"], OPT["pn"]
    NB = [6 * BANK + 64 * j if j < cut else 7 * BANK + 64 * j for j in range(4)]

    def H(name, h, base=0):
        return A(name, base, base + F) if h is None else A(name, base + BANK * h, base + BANK * h + BANK)

    def parts(t, tag, s=""):
        for h in ([None] if tag in OPT["whole"] or tag + str(s) in OPT["whole"] else [0, 1]):
            at(t, tag + str(s) + ("" if h is None else "ab"[h]))
            yield h

    def halves(t, tag, s=""):
        for h in range(2):
            at(t, tag + str(s) + "ab"[h])
            yield h

    def xo(t, h=None):
        return H("xa%d" % t, h)

    def xs(t, h=None):
        return H("xw%d" % t, h, o)

    def gx(t, lst, j):
        return ("ind", A("xw%d" % t, 0, W), A(lst, 64 * j, 64 * j + 64))

    def ps(c0, n):
        return A("ps", c0, c0 + n)

    def M(name):
        return A(name, 0, 128)

    def group(out, terms, start=True):
        return [(out, M(m) if isinstance(m, str) else m, a, start and i == 0, i == len(terms) - 1) for i, (m, a) in enumerate(terms)]

    def digits(t, k):
        nm, hi = A("nmf", 64 * k, 64 * k + 64), A("dg", 2 * k, 512, 8)
        at(t, "dh%d" % k)
        if k == 3:
            cp(hi, nm)
        else:
            act(hi, nm, "Copy")
        at(t, "dl%d" % k)
        tt(A("dg", 2 * k + 1, 512, 8), nm, hi, "subtract")

    def rows(t, u):
        at(t, "turn")
        add("dve", "tr", (A("dt", 0, 512, idx=(slice(0, 128),)), A("dg", 0, 512)), [A("dg", 0, 512)], [A("dt", 0, 512)])
        for h in halves(t, "row"):
            blk = slice(8 * h, 8 * h + 8)
            it = []
            for c2 in range(4):
                out = A("ps", UB + BANK * h, UB + BANK * h + BANK, idx=(slice(0, 128), blk, c2), n=128)
                it += group(out, [(A("rs", 144 * c2 + 16 * (1 - g0), 144 * c2 + 16 * (1 - g0) + 128),
                                   A("dt", 256 * h, 256 * h + 256, idx=(slice(0, 128), blk, g0), n=128)) for g0 in range(2)])
            mm(it)
        for h in parts(t, "rc"):
            act(H("nw%d" % u, h, o), H("ps", h, UB), "Copy")
        for h in parts(t, "ns"):
            a = H("nw%d" % u, h, o)
            send(a, "an%d_%d" % (u, h or 0))
            arrive("nw%d" % u, a[1] - o, a[2] - o, "an%d_%d" % (u, h or 0))

    def one(tag):
        at(-1, tag)

    one("load")
    dma("sp", xo(0), A("x", 0, F), "lx")
    dma("act", A("nbi", 0, 256), A("nb", 0, 256), "ln")
    dma("sp", xs(0), A("x", 0, F), "cx0_0")
    dma("sp", A("mixb", 0, F, 1, 0, 16), A("mix", 0, F, 1, 0, 16), "lm")
    iota(A("i1", 0, 144), [[-1, 144]], 128, 1)
    iota(A("i4", 0, 256), [[0, 4], [16, 64]], o, 1)
    send(xo(0), "ax0_0", xs(0))
    arrive("xw0", 0, F, "ax0_0")
    ms(A("aw", 0, 864), 0.0)
    ms(A("bb", 0, 136), 0.0)
    ts(A("pc", 4, 8), A("i1", 0, 32, 8), 31, 3, "bitwise_and", "arith_shift_right")
    ts(M("ib"), M("i1"), 128.0, None, "is_equal")
    ts(A("pcf", 4, 8), A("pc", 4, 8), 0.0, None, "is_equal")
    ts(M("i3"), M("i1"), 15, None, "bitwise_and")
    for c2 in range(4):
        ts(A("rs", 144 * c2, 144 * c2 + 144), A("i1", 0, 144), 112.0 + 8 * c2, A("pcf", 4 + c2, 5 + c2), "is_equal", "mult")
    act(M("nib"), M("ib"), "Copy", -1.0)
    act(M("hb"), M("ib"), "Copy", 0.5)
    one("list")
    cp(A("nmf", 0, 256), A("nbi", 0, 256))
    one("off")
    cp(A("off", 0, 256), A("nbi", 0, 256))
    for k in range(4):
        digits(-1, k)
    rows(-1, 0)
    one("more")
    ts(M("i5"), M("i1"), 1, None, "arith_shift_right")
    ts(M("i6"), M("i1"), 4, None, "arith_shift_right")
    ts(A("pc", 0, 1), A("i1", 0, 1), 112, None, "bitwise_and")
    ts(M("bm8"), M("i3"), 0.0, -0.125, "is_equal", "mult")
    for k in range(4):
        ts(A("aw", 144 * k + 15, 144 * k + 143, 16), A("i5", 2 * k, 128, 16), 64.0, None, "is_equal")
    ts(A("aw", 576 + 15, 576 + 143, 16), A("i6", 0, 128, 16), 8.0, None, "is_equal")
    ts(A("aw", 720 + 15, 720 + 143, 16), A("i6", 0, 128, 16), 8.0, 0.5, "is_equal", "mult")
    ms(A("mh", 0, 64), -0.5)
    cp(A("pcf", 0, 1), A("pc", 0, 1))
    tt(M("mf"), M("bm8"), M("ib"), "add")
    ts(A("own", 0, 256), A("i4", 0, 256), A("pcf", 0, 1), None, "subtract")
    one("mats")
    act(M("e8"), M("bm8"), "Copy", -1.0)
    act(M("n16"), M("ib"), "Copy", -16.0)
    act(M("idf"), M("ib"), "Copy")
    act(M("nidf"), M("ib"), "Copy", -1.0)
    act(A("bb", 7, 135, 8), A("bm8", 0, 16), "Copy", -8.0)
    act(M("mb"), M("mf"), "Copy")
    act(M("nmb"), M("mf"), "Copy", -1.0)
    act(M("nmtx"), M("mf"), "Copy", -1.0)

    def d_open(t, u):
        for s in range(2):
            if OPT["pesub"][u][s] == 1:
                for h in halves(t, "do", s):
                    mm([(H("ps", h, F * s), M("nib" if NARROW[u] else "nidf"), xo(u, h), True, False)])

    d_open(-1, 0)

    for t in range(ROUNDS):
        last = t == ROUNDS - 1
        b = "b" if NARROW[t] else ""
        pos, neg = ("ib", "nib") if NARROW[t] else ("idf", "nidf")
        prod, upe, stage = OPT["prod"][t], OPT["upe"][t], OPT["stage"][t]
        P = [lambda h: H("ps", h), lambda h: H("ps", h, F)]

        for s in range(2):
            at(t, "d%d" % s)
            tt(H("ds" + b, None, F * s), gx(t, "off", SN[s]), xo(t), "subtract")
            at(t, "as%d" % s)
            act(H("adv", None, F * SN[s]), H("ds" + b, None, F * s), "Abs")
            at(t, "v%d" % s)
            if OPT["pesub"][t][s] == 2:
                tt(H("dp", None, F * s), gx(t, "off", PN[s]), xo(t), "subtract")
                for h in halves(t, "dx", s):
                    mm([(P[s](h), M(pos), H("dp", h, F * s), True, True)])
            elif OPT["pesub"][t][s]:
                act(H("dp" + b, None, F * s), gx(t, "off", PN[s]), "Copy")
                for h in halves(t, "dx", s):
                    mm([(P[s](h), M(pos), H("dp" + b, h, F * s), False, True)])
            else:
                tt(H("dp", None, F * s), gx(t, "off", PN[s]), xo(t), "subtract")
                for h in parts(t, "dc", s):
                    act(P[s](h), H("dp", h, F * s), "Copy")
            if PN[s] not in prod:
                for h in parts(t, "ap", s):
                    act(H("adv", h, F * PN[s]), P[s](h), "Abs")
        at(t, "ext")
        act(A("nmf", 256, 448), A("nmf", 0, 192), "Copy")

        for h in halves(t, "zo"):
            if last:
                mm([(H("ps", h, UB), M("idf"), xo(t, h), True, False)])
            else:
                mm([(H("ps", h, UB), A("e8", 0, 128, 1, 0, 16), A("mixb", BANK * h, BANK * h + BANK, 1, 0, 16), True, False),
                    (H("ps", h, UB), M("mb" if b else "mf"), xo(t, h), False, False)])
        for h in parts(t, "lo1"):
            tt(H("lo" + b, h), P[0](h), H("ds" + b, h), "min")
        for h in parts(t, "hi2"):
            tt(H("hi" + b, h), P[1](h), H("ds" + b, h, F), "max")
        if OPT["comp1"][t]:
            for h in halves(t, "hi1"):
                mm(group(P[0](h), [(pos, H("dp" + b, h)), (neg, xo(t, h)), (pos, H("ds" + b, h)), (neg, H("lo" + b, h))]))
            for h in halves(t, "lo2"):
                mm(group(P[1](h), [(pos, H("dp" + b, h, F)), (neg, xo(t, h)), (pos, H("ds" + b, h, F)), (neg, H("hi" + b, h))]))
        else:
            for h in parts(t, "hi1"):
                tt(P[0](h), P[0](h), H("ds" + b, h), "max")
            for h in parts(t, "lo2"):
                tt(P[1](h), P[1](h), H("ds" + b, h, F), "min")
        for h in parts(t, "L"):
            tt(H("lo" + b, h), P[1](h), H("lo" + b, h), "max")
        for h in parts(t, "H"):
            tt(H("hi" + b, h) if OPT["comp3"][t] else P[0](h), P[0](h), H("hi" + b, h), "min")
        if OPT["comp3"][t]:
            for h in halves(t, "lh"):
                mm(group(P[1](h), [(pos, H("lo" + b, h)), (neg, H("hi" + b, h))]))
            for h in parts(t, "r"):
                act(H("ds" + b, h), P[1](h), "Relu")
            for h in halves(t, "p"):
                mm(group(P[0](h), [(pos, H("lo" + b, h)), (neg, H("ds" + b, h))]))
            for h in halves(t, "q"):
                mm(group(P[1](h), [(neg, H("hi" + b, h)), (neg, H("ds" + b, h))]))
            for h in parts(t, "rp"):
                act(H("pp" + b, h), P[0](h), "Relu")
            for h in parts(t, "rq"):
                act(H("qq" + b, h), P[1](h), "Relu")
        else:
            for h in parts(t, "p"):
                tt(H("pp", h), P[0](h), H("lo" + b, h), "min")
            for h in parts(t, "q"):
                tt(H("qq", h), P[0](h), H("lo" + b, h), "max")
            for h in parts(t, "rp"):
                act(H("pp" + b, h), H("pp", h), "Relu")
            for h in parts(t, "rq"):
                act(H("qq" + b, h), H("qq", h), "Relu", -1.0)
        zp, zn = ("idf", "nidf") if last else (("mb", "nmb") if b else ("mf", "nmtx"))
        for h in halves(t, "zc"):
            mm(group(H("ps", h, UB), [(zp, H("pp" + b, h)), (zn, H("qq" + b, h))], False))
        for h in halves(t, "xn"):
            if last:
                act(H("hi", h), H("ps", h, UB), "Square")
                dma("sp", H("ye", h), H("hi", h), "oe%d" % h)
            else:
                act(xo(t + 1, h), H("ps", h, UB), "Relu")
                send(xo(t + 1, h), "ax%d_%d" % (t + 1, h), xs(t + 1, h))
                dma("sp", xs(t + 1, h), xo(t + 1, h), "cx%d_%d" % (t + 1, h))
                arrive("xw%d" % (t + 1), BANK * h, BANK * h + BANK, "ax%d_%d" % (t + 1, h))

        for j in range(4):
            at(t, "c%d" % j)
            act(H("cg", None, F * j), ("ind", A("nw%d" % t, 0, W), A("off", 64 * j, 64 * j + 64)), "Copy")
            at(t, "cl%d" % j)
            k = (j + t) % 4
            mm(group(ps(CB + 64 * j, 64), [(A("aw", 144 * k + 15 - m, 144 * k + 143 - m), A("cg", F * j + m, F * j + F, 16)) for m in range(16)]))
        for j, j1 in OPT["cof"]:
            at(t, "cof%d" % j)
            cp(A("cof", 64 * j, 64 * j1), ps(CB + 64 * j, 64 * (j1 - j)))
        at(t, "csb")
        act(A("csb", 0, 192), ps(CB, 192), "Copy")
        c = ps(CB, 256)
        for i in range(4):
            at(t, "e%d" % i)
            tt(A("eq", 256 * i, 256 * i + 256), c, A("nmf", 64 * i, 64 * i + 256) if i else A("own", 0, 256), "is_equal")
        at(t, "dlt")
        tt(A("dlt", 0, 256), c, A("nmf", 0, 256), "subtract")
        for i, e in ((1, 1024), (2, 1216), (3, 1344)):
            at(t, "f%d" % i)
            n = 256 - 64 * i
            tt(A("eq", e, e + n), ps(CB + 64 * i, n), A("csb", 0, n), "is_equal")
        for j in range(4):
            s, base = j % 2, stage[j]
            if j in prod:
                v = F * PN.index(j)
                at(t, "u%d" % j)
                tt(H("dub", None, F * s), gx(t, "cof", j), H("dpb", None, v), "subtract")
                for h in halves(t, "uo", j):
                    mm([(H("ps", h, base), M("ib"), H("dpb", h, v), True, False), (H("ps", h, base), M("nib"), xo(t, h), False, False)])
                for h in halves(t, "ux", j):
                    mm([(H("ps", h, base), M("hb"), H("dub", h, F * s), False, True)])
                for h in parts(t, "lt", j):
                    tt(H("near", h, F * j), H("ps", h, base), H("dub", h, F * s), "mult")
                at(t, "neg%d" % j)
                if j in OPT["sign"]:
                    act(H("near", None, F * j), H("near", None, F * j), "Sign", -1.0, -1.0 / 256)
                else:
                    ts(H("near", None, F * j), H("near", None, F * j), 0.0, None, "is_lt")
            else:
                at(t, "u%d" % j)
                if j in upe:
                    act(H("ds" + b, None, F * s), gx(t, "cof", j), "Copy")
                    for h in halves(t, "uo", j):
                        mm([(H("ps", h, base), M(neg), xo(t, h), True, False)])
                    for h in halves(t, "ux", j):
                        mm([(H("ps", h, base), M(pos), H("ds" + b, h, F * s), False, True)])
                    for h in parts(t, "au", j):
                        act(H("ps", h, base), H("ps", h, base), "Abs")
                elif j in OPT["udma"][t]:
                    u, sem = H("dp", None, F * s), "ga%d_%d" % (t, s)
                    act(u, gx(t, "cof", j), "Copy", -1.0)
                    at(t, "ux%d" % j)
                    add("pool", "gdma", (u, xo(t), sem), [u, xo(t)], [u], (sem, 16))
                    for h in parts(t, "au", j):
                        act(H("ps", h, base), H("dp", h, F * s), "Abs")
                else:
                    tt(H("du", None, F * s), gx(t, "cof", j), xo(t), "subtract")
                    for h in parts(t, "au", j):
                        act(H("ps", h, base), H("du", h, F * s), "Abs")
                for h in parts(t, "lt", j):
                    tt(H("near", h, F * j), H("ps", h, base), H("adv", h, F * j), "is_lt")
            at(t, "n%d" % j)
            signs = j in prod and j in OPT["sign"]
            w = 720 if signs else 576
            mm(group(ps(NB[j], 64), [("n16", A("eq", e, e + 64)) for e in EQ[j]] + [("n16", A("mh", 0, 64))] * signs
                     + [(A("aw", w + 15 - m, w + 143 - m), A("near", F * j + m, F * j + F, 16)) for m in range(16)]))
        if last:
            at(t, "sum")
            mm(group(ps(BANK, 128), [(A("bb", 7 - i, 135 - i), A("hi", 128 * i, 128 * i + 128)) for i in range(8)]))
            at(t, "yd")
            act(M("yds"), ps(BANK, 128), "Copy")
            dma("sp", A("yd", 0, F, 1, 0, 16), M("yds"), "od")
        else:
            d_open(t, t + 1)
        for k0, k1 in ((0, cut), (cut, 4)):
            n, nm = ps(NB[k0], 64 * (k1 - k0)), A("nmf", 64 * k0, 64 * k1)
            at(t, "ge%d" % k0)
            ts(n, n, 8.5, None, "is_ge")
            at(t, "mul%d" % k0)
            tt(n, n, A("dlt", 64 * k0, 64 * k1), "mult")
            at(t, "new%d" % k0)
            tt(nm, n, nm, "add")
            at(t, "off%d" % k0)
            if last:
                dma("sp", A("yn", 64 * k0, 64 * k1), nm, "on%d" % (k0 > 0))
            else:
                cp(A("off", 64 * k0, 64 * k1), nm)
                for k in range(k0, k1):
                    digits(t, k)
        if not last:
            rows(t, t + 1)
    return ops


def width(a):
    if a[0] == "ind":
        return 16 * (a[2][2] - a[2][1])
    return a[7] or len(range(a[1], a[2], a[3]))


def size(a):
    return 2 if a[0] in SCRATCH and SCRATCH[a[0]][2] in ("bfloat16", "uint16") else 4


ORDER = {
    "start": "load list do1b dh2 dh1 dh3 dh0 dl1 dl0 dl3 dl2 turn off more do0a rowb rowa do1a rcb rca do0b ns mats",
    "narrow": "zoa v0 v1 d0 d1 as1 as0 c1 dx0a dx0b c0 dx1a lo1 dx1b zob hi2 hi1 lo2 cl1 H L cof1 cl0 uo1a c2 cl2 c3 qa pa rpa rqa u1 pb cof0 qb cl3 rpb rqb ux1a zca xna zcb u0 cof2 dlt uo1b uo0b u2 csb ext xnb au2a e1 uo0a ux0b ux1b au2b ux0a e2 e3 f1 lt2a lt2b u3 f2 uo3a ux3a lt1 uo3b ux3b e0 n2 neg1 lt0 n1 f3 au3b au3a neg0 n0 lt3a lt3b ge0 mul0 new0 n3 dh1 dh0 dh2 do1a do1b do0b do0a ge3 off0 mul3 dl1 v0+ new3 dl0 dh3 dl2 dl3 turn rowa rowb rca off3 rcb ns",
    "wide": "dx0a ext d0 v1 dx0b as0 d1 ap0 dx1b dx1a as1 lo1 ap1 hi1 c0 zob c2 c3 cl0 zoa hi2 lo2 H L cof0 c1 pb cl2 rpb qb cl3 pa rqb cof2 u3 cl1 u0 cof1 qa e2 u1 e0 e1 ux3 dlt e3 rpa rqa au0a au0b zcb xnb lt0 zca u2 au1b csb au1a n0 lt1 xna au2b au2a f1 lt2b lt2a f3 do0b sum au3b f2 lt3b au3a n1 n2 lt3a ge0 mul0 new0 yd dh1 dh0 n3 ge3 do0a off0 v0 mul3 dh2 dl1 new3 dl2 dh3 v0+ dl0 dl3 turn rowa rca rowb rcb off3 ns",
}


def arrange(ops):
    if not ORDER:
        return ops
    steps = {}
    for op in ops:
        steps.setdefault(op["tag"], []).append(op)
    out = []
    for t in range(-1, ROUNDS):
        for name in ORDER["start" if t < 0 else "narrow" if NARROW[t] else "wide"].split():
            out += steps.pop((t + 1, name[:-1]) if name[-1] == "+" else (t, name), [])
    assert not steps
    return out


def meet(a, b):
    return a[0] < b[1] and b[0] < a[1] and not (a[2] == b[2] > 1 and (a[0] - b[0]) % a[2])


def touches(op):
    return sorted(set([(a[0], a[1:4], False) for a in op["reads"]] + [(a[0], a[1:4], True) for a in op["writes"]]))


def orders(ops):
    seen = {}
    for i, op in enumerate(ops):
        deps = set()
        acc = touches(op)
        for name, c, w in acc:
            for k, d, dw in seen.get(name, []):
                other = ops[k]["eng"]
                if name == "ps" and other != op["eng"]:
                    hit = c[0] // BANK <= (d[1] - 1) // BANK and d[0] // BANK <= (c[1] - 1) // BANK
                elif name == "ps" and other == "pe":
                    hit = False
                else:
                    hit = (w or dw) and meet(c, d)
                if hit:
                    deps.add(k)
        for name, c, w in acc:
            lst = seen.setdefault(name, [])
            if w and name != "ps":
                lst[:] = [e for e in lst if not (c[0] <= e[1][0] and e[1][1] <= c[1] and (c[2] == 1 or (c[2] == e[1][2] and c[0] == e[1][0])))]
            lst.append((i, c, w))
            if name == "ps" and len(lst) > 400:
                del lst[:100]
        best = {}
        for k in deps:
            key = ops[k]["token"][0] if ops[k]["token"] else ops[k]["eng"]
            if ops[k]["kind"] == "send":
                continue
            best[key] = max(best.get(key, -1), k)
        op["deps"] = best
    done = {}
    for i, op in enumerate(ops):
        have = done.setdefault(op["eng"], {})
        op["deps"] = {key: k for key, k in op["deps"].items() if have.get(key, -1) < k}
        have.update(op["deps"])
    for op in ops:
        op["signal"] = False
    for op in ops:
        if op["kind"] != "arr":
            for k in op["deps"].values():
                ops[k]["signal"] = True
    return ops


def rank_program(g, core, T, topo):
    rank = T.rank_of(core)
    if rank is None:
        return
    peers = [c for c in T.cores if c != core]
    mask = topo.mask(core, peers[0])
    for c in peers:
        mask &= topo.mask(core, c)
    lanes = len([e for e in topo.engines(core, peers[0]) if mask >> e & 1])
    dst_ids = [DstId(rid=topo.addr(c)[0], pnc=topo.addr(c)[1]) for c in peers]
    queue = {"pe": g.tensor, "dve": g.vector, "act": g.scalar, "sp": g.sync, "pool": g}
    alu = {"add": AluOpType.add, "subtract": AluOpType.subtract, "mult": AluOpType.mult, "max": AluOpType.max,
           "min": AluOpType.min, "is_ge": AluOpType.is_ge, "is_lt": AluOpType.is_lt, "is_equal": AluOpType.is_equal,
           "bitwise_and": AluOpType.bitwise_and, "arith_shift_right": AluOpType.arith_shift_right}
    fun = {"Copy": ActivationFunctionType.Copy, "Abs": ActivationFunctionType.Abs, "Relu": ActivationFunctionType.Relu,
           "Square": ActivationFunctionType.Square, "Sign": ActivationFunctionType.Sign}

    def ap(a):
        if not isinstance(a, tuple):
            return a
        if a[0] == "ind":
            return ap(a[1]).indirect(ap(a[2]))
        name, c0, c1, step, p0, p1, idx, n = a
        if name == "ps":
            if UB <= c0 < UB + F:
                return T.pu[idx] if idx else T.pu[p0:p1, (c0 - UB) // 64:(c1 - UB) // 64]
            name, c0, c1 = ("pa", c0, c1) if c0 < UB else ("pl", c0 - UB - F, c1 - UB - F)
        if idx:
            return T[name][idx]
        return T[name][p0:p1, c0:c1] if step == 1 else T[name][p0:p1, c0:c1:step]

    ops = orders(arrange(plan(rank)))
    count = {"pe": 0, "dve": 0, "act": 0, "pool": 0}
    sent = 0
    stores = []
    for op in ops:
        kind, a = op["kind"], op["args"]
        if kind == "arr":
            op["mark"] = (a[0], lanes * len(peers))
            continue
        q = queue[op["eng"]]
        for k in op["deps"].values():
            q.wait_ge(T.sem[ops[k]["mark"][0]], ops[k]["mark"][1])
        if kind == "dma":
            q.dma_start(ap(a[0]), ap(a[1])).then_inc(T.sem[a[2]], 16)
            op["mark"] = op["token"]
            if not op["signal"]:
                stores.append(a[2])
            continue
        if kind == "gdma":
            g.dma_start(ap(a[0]), ap(a[1]), accum_op=AluOpType.add).then_inc(T.sem[a[2]], 16)
            op["mark"] = op["token"]
            continue
        if kind == "send":
            g.remote_dma_fused([RemoteDMATransfer(dst_ids=dst_ids, dma_engine_mask=mask, remote_sem=T.sem[a[1]],
                                                  src=ap(a[0]), dsts=[ap(a[2]) for c in peers])], local_sem=T.sem.sent)
            sent += lanes
            continue
        if kind == "tt":
            ins = q.tensor_tensor(ap(a[0]), ap(a[1]), ap(a[2]), alu[a[3]])
        elif kind == "ts":
            if a[5] is None:
                ins = q.tensor_scalar(ap(a[0]), ap(a[1]), ap(a[2]), None, alu[a[4]])
            else:
                ins = q.tensor_scalar(ap(a[0]), ap(a[1]), ap(a[2]), ap(a[3]), alu[a[4]], alu[a[5]])
        elif kind == "cp":
            ins = q.tensor_copy(ap(a[0]), ap(a[1]))
        elif kind == "tr":
            ins = q.transpose(ap(a[0]), ap(a[1]))
        elif kind == "ms":
            ins = q.memset(ap(a[0]), a[1])
        elif kind == "act":
            ins = q.activation(ap(a[0]), ap(a[1]), fun[a[2]], bias=a[4], scale=a[3])
        elif kind == "iota":
            ins = q.iota(ap(a[0]), a[1], a[2], a[3])
        else:
            for out, lhs, rhs, start, stop in a:
                ins = q.matmul(ap(out), ap(lhs), ap(rhs), start, stop)
        if op["signal"]:
            count[op["eng"]] += 1
            ins.then_inc(T.sem[op["eng"]], 1)
            op["mark"] = (op["eng"], count[op["eng"]])
    for s in stores:
        g.sync.wait_ge(T.sem[s], 16)
    g.wait_ge(T.sem.sent, sent)
